import numpy as np
import ml_dtypes


def mxq(x, axis, fmt="e4m3"):
    dtype, down = {"e4m3": (ml_dtypes.float8_e4m3fn, 7), "e5m2": (ml_dtypes.float8_e5m2, 14)}[fmt]
    v = np.moveaxis(np.asarray(x, np.float32).astype(ml_dtypes.bfloat16).astype(np.float64), axis, -1)
    blocks = v.reshape(v.shape[:-1] + (-1, 32))
    amax = np.abs(blocks).max(-1, keepdims=True)
    byte = np.maximum(np.where(amax > 0, np.frexp(amax)[1] - 1 + 127, 0) - down, 1)
    scale = np.exp2(byte - 127.0)
    codes = (blocks / scale).astype(np.float32).astype(dtype).astype(np.float64)
    return np.moveaxis((codes * scale).reshape(v.shape), -1, axis)


WIDE = False


def mx_kscale(k):
    if not WIDE:
        return np.ones(k)
    levels = np.array([10, -10, 5, -5, 0])
    if k % 512:
        return np.exp2(np.random.permutation(np.resize(levels, k // 32))).repeat(32)
    a = np.empty((k // 512, 16))
    for p in range(k // 512):
        a[p, :8] = np.random.permutation(np.resize(levels, 8))
        for g in range(8):
            far = levels[np.abs(levels - a[p, g]) >= 10]
            a[p, g + 8] = far[np.random.randint(len(far))]
    return np.exp2(a.ravel()).repeat(32)


def f64(x):
    return np.asarray(x).astype(np.float64)


def striped(idx):
    return np.tile(idx.reshape(-1, 16).T, (8, 1)).astype(np.uint16)


def unstriped(offs):
    return offs[:16].T.reshape(-1).astype(np.int64)


E2M1 = np.array([0.0, 0.5, 1.0, 1.5, 2.0, 3.0, 4.0, 6.0, -0.0, -0.5, -1.0, -1.5, -2.0, -3.0, -4.0, -6.0])


def pack_weight(w, fmt):
    k, n = w.shape
    w = f64(np.asarray(w, np.float32).astype(ml_dtypes.bfloat16)).reshape(k // 32, 32, n)
    amax = np.abs(w).max(1)
    if fmt == "e4m3":
        byte = np.frexp(amax)[1] - 1 + 127 - 7
    else:
        mant, ex = np.frexp(amax / 6.0)
        byte = np.where(mant > 0.5, ex, ex - 1) + 127
    byte = np.clip(np.where(amax > 0, byte, 1), 1, 254)
    scaled = (w * np.exp2(127.0 - byte)[:, None, :]).reshape(k, n).astype(np.float32)
    by_word = np.ascontiguousarray(scaled.reshape(k // 512, 128, 4, n).transpose(0, 1, 3, 2))
    if fmt == "e4m3":
        words = by_word.astype(ml_dtypes.float8_e4m3fn).view(np.uint8)
    else:
        c = by_word.astype(ml_dtypes.float4_e2m1fn).view(np.uint8) & 0xF
        words = (c[..., 0::2] | (c[..., 1::2] << 4)).reshape(k // 512, 128, 2 * n)
    return np.ascontiguousarray(words), np.ascontiguousarray(byte.astype(np.uint8).reshape(k // 512, 16, n))


def unpack_weight(words, scales, fmt):
    g, _, n = scales.shape
    words = np.ascontiguousarray(words).reshape(g, 128, n, -1)
    if fmt == "e4m3":
        vals = words.view(ml_dtypes.float8_e4m3fn).astype(np.float64)
    else:
        nib = np.empty((g, 128, n, 4), np.uint8)
        nib[..., 0::2] = words & 0xF
        nib[..., 1::2] = words >> 4
        vals = E2M1[nib]
    vals = vals * np.repeat(np.exp2(scales.astype(np.float64) - 127.0), 8, axis=1)[..., None]
    return vals.transpose(0, 1, 3, 2).reshape(g * 512, n)


def gelu(v):
    return 0.5 * v * (1.0 + np.tanh(np.sqrt(2.0 / np.pi) * (v + 0.044715 * v**3)))


K, K2, H, N, T, T2, S = 1024, 512, 512, 384, 4096, 2048, 1024

def setup_inputs():
    n = np.random.standard_normal
    s, s2 = mx_kscale(K)[:, None], mx_kscale(K2)[:, None]
    u = mx_kscale(H)[:, None]
    tab_words, tab_scales = pack_weight(n((K, T)) * s, "e4m3")
    tab2_words, tab2_scales = pack_weight(n((K2, T2)) * s2, "e4m3")
    wfx_words, wfx_scales = pack_weight(n((K2, H)) / np.sqrt(K2) / s2, "e2m1")
    wfy_words, wfy_scales = pack_weight(n((K2, H)) / np.sqrt(K2) / s2, "e2m1")
    wt_words, wt_scales = pack_weight(n((H, N)) / np.sqrt(H) / u, "e4m3")
    return {
        "tab_words": tab_words, "tab_scales": tab_scales,
        "tab2_words": tab2_words, "tab2_scales": tab2_scales,
        "offs": striped(np.random.permutation(T)[:S]),
        "offs2": striped(np.random.permutation(T2)[:S]),
        "wex": (n((K, H)) / np.sqrt(K) / s * u.T).astype(np.float32),
        "wey": (n((K, H)) / np.sqrt(K) / s * u.T).astype(np.float32),
        "wfx_words": wfx_words, "wfx_scales": wfx_scales,
        "wfy_words": wfy_words, "wfy_scales": wfy_scales,
        "wt_words": wt_words, "wt_scales": wt_scales,
        "tl": n(N).astype(np.float32),
    }

def reference(tab_words, tab_scales, tab2_words, tab2_scales, offs, offs2, wex, wey,
              wfx_words, wfx_scales, wfy_words, wfy_scales, wt_words, wt_scales, tl):
    v = unpack_weight(tab_words, tab_scales, "e4m3")[:, unstriped(offs)]
    v2 = unpack_weight(tab2_words, tab2_scales, "e4m3")[:, unstriped(offs2)]
    ex = mxq(f64(wex), 0, "e4m3").T @ v
    ey = mxq(f64(wey), 0, "e4m3").T @ v
    fx = unpack_weight(wfx_words, wfx_scales, "e2m1").T @ v2
    fy = unpack_weight(wfy_words, wfy_scales, "e2m1").T @ v2
    h = ex * fy - ey * fx
    y = unpack_weight(wt_words, wt_scales, "e4m3").T @ mxq(h, 0, "e4m3")
    return y - f64(tl)[:, None]

@@ -1,0 +1,251 @@
+from contextlib import ExitStack
+
+import concourse.mybir as mybir
+
+K, K2, H, N, T, T2, S = 1024, 512, 512, 384, 4096, 2048, 1024
+FLOPS = 2 * S * (2 * K * H + 2 * K2 * H + H * N)
+
+F32 = mybir.dt.float32
+BF16 = mybir.dt.bfloat16
+I32 = mybir.dt.int32
+U32 = mybir.dt.uint32
+U16 = mybir.dt.uint16
+U8 = mybir.dt.uint8
+FP8X4 = mybir.dt.float8_e4m3fn_x4
+FP4X4 = mybir.dt.float4_e2m1fn_x4
+ALU = mybir.AluOpType
+ACT = mybir.ActivationFunctionType
+
+P = 128
+PACK = 4
+C = 128
+CHUNKS = S // C
+HALF = S // 2
+NT = N // P
+F_BANKS = ((0, 1, 2, 3, 4, 0, 1, 2), (0, 1, 2, 3, 4, 5, 6, 7))
+E_BANKS = ((5, 6, 7, 0, 1, 2, 3, 4), (5, 6, 7, 3, 5, 6, 7, 3))
+Y_BANKS = (4, 0, 1, 2, 4, 0, 1, 2)
+STORE_GROUPS = ((0, 2), (2, 4), (4, 6), (6, 7), (7, 8))
+
+
+def tile_list_edge_field_torque_kernel(
+    tc, tab_words, tab_scales, tab2_words, tab2_scales, offs, offs2, wex, wey,
+    wfx_words, wfx_scales, wfy_words, wfy_scales, wt_words, wt_scales, tl, out,
+):
+    nc = tc.nc
+    with ExitStack() as ctx:
+        keep = ctx.enter_context(tc.tile_pool(name="keep", bufs=1))
+        psum = ctx.enter_context(tc.psum_pool(name="psum", bufs=1))
+        banks = [psum.tile([P, PACK, C], F32, name="bank%d" % b) for b in range(8)]
+
+        def sb(name, shape, dtype):
+            return keep.tile(shape, dtype, name=name, align_bytes=64)
+
+        idx = keep.tile([P, S // 16], U16, name="idx")
+        idx2 = keep.tile([P, S // 16], U16, name="idx2")
+        v_words = [sb("v_words%d" % a, [P, T], I32) for a in range(2)]
+        v_scales = sb("v_scales", [P, T // 4], I32)
+        v2_words = sb("v2_words", [P, T2], I32)
+        v2_scales = sb("v2_scales", [P, T2 // 4], I32)
+        gv_words = [sb("gv_words%d" % a, [P, S], U32) for a in range(2)]
+        gv_scales = sb("gv_scales", [P, S], U8)
+        gv2_words = sb("gv2_words", [P, S], U32)
+        gv2_scales = sb("gv2_scales", [P, S], U8)
+        wf_words_raw = [sb("wf_words_raw%d" % w, [P, H // 2], I32) for w in range(2)]
+        wf_scales_raw = [sb("wf_scales_raw%d" % w, [P, H // 4], I32) for w in range(2)]
+        wf_words = [sb("wf_words%d" % w, [P, 2 * H], U8) for w in range(2)]
+        wf_scales = [sb("wf_scales%d" % w, [P, H], U8) for w in range(2)]
+        we_raw = [[sb("we_raw%d%d" % (w, a), [P, PACK, H], F32) for a in range(2)] for w in range(2)]
+        we_bf = [[sb("we_bf%d%d" % (w, a), [P, PACK * H], BF16) for a in range(2)] for w in range(2)]
+        we_words = [[sb("we_words%d%d" % (w, a), [P, H], U32) for a in range(2)] for w in range(2)]
+        we_scales = [[sb("we_scales%d%d" % (w, a), [P, H], U8) for a in range(2)] for w in range(2)]
+        wt_w = sb("wt_w", [P, N], I32)
+        wt_s = sb("wt_s", [P, N // 4], I32)
+        tl_col = sb("tl_col", [P, NT], F32)
+        neg_tl = sb("neg_tl", [P, NT], F32)
+        f_sb = [[sb("f_sb%d%d" % (w, c), [P, C * PACK], F32) for c in range(CHUNKS)] for w in range(2)]
+        prod = [sb("prod%d" % w, [P, S * PACK], F32) for w in range(2)]
+        h_bf = sb("h_bf", [P, S * PACK], BF16)
+        h_words = sb("h_words", [P, S], U32)
+        h_scales = sb("h_scales", [P, S], U8)
+        y_sb = sb("y_sb", [P, NT, S], F32)
+
+        def words_of(dram, a):
+            return dram[a].rearrange("p t i -> p (t i)").bitcast(I32)
+
+        def load_scale_rows(engine, tile, dram, a):
+            for q in range(4):
+                first = 32 * q + 4 * a
+                engine.dma_start(out=tile[first : first + 4, :], in_=dram[a, 4 * q : 4 * q + 4, :].bitcast(I32))
+
+        def fill_scale_rows(tile, dram, quadrants):
+            for q in quadrants:
+                nc.sync.dma_start(
+                    out=tile[32 * q : 32 * (q + 1), :],
+                    in_=dram[0, 4 * q : 4 * q + 4, :].bitcast(I32).partition_broadcast(8),
+                )
+
+        def load_we(w, a, c0, c1):
+            rows = (wex, wey)[w][512 * a : 512 * (a + 1), c0:c1]
+            nc.sync.dma_start(out=we_raw[w][a][:, :, c0:c1], in_=rows.rearrange("(p j) c -> p j c", j=PACK))
+
+        for tile in (wf_scales_raw[1], wf_scales_raw[0], wt_s, v_scales):
+            nc.vector.memset(tile[:], 0)
+
+        load_scale_rows(nc.gpsimd, wf_scales_raw[1], wfy_scales, 0)
+        load_scale_rows(nc.gpsimd, wf_scales_raw[0], wfx_scales, 0)
+        load_scale_rows(nc.gpsimd, wt_s, wt_scales, 0)
+        nc.sync.dma_start(idx2[:], offs2)
+        fill_scale_rows(v2_scales, tab2_scales, range(4))
+        nc.sync.dma_start(out=wf_words_raw[1][:], in_=wfy_words[0].bitcast(I32))
+        nc.sync.dma_start(out=v2_words[:], in_=words_of(tab2_words, 0))
+        nc.sync.dma_start(out=v_words[0][:], in_=words_of(tab_words, 0))
+        nc.sync.dma_start(idx[:], offs)
+        load_scale_rows(nc.sync, v_scales, tab_scales, 0)
+        load_we(0, 0, 0, H)
+        nc.sync.dma_start(out=wf_words_raw[0][:], in_=wfx_words[0].bitcast(I32))
+        load_scale_rows(nc.sync, v_scales, tab_scales, 1)
+        nc.sync.dma_start(out=v_words[1][:], in_=words_of(tab_words, 1))
+        load_we(0, 1, 0, H // 2)
+        load_we(0, 1, H // 2, H)
+        load_we(1, 0, 0, H)
+        with nc.allow_non_contiguous_dma(reason="one value of tl to a partition"):
+            nc.sync.dma_start(out=tl_col[:], in_=tl.rearrange("(c p) -> p c", p=P))
+        load_we(1, 1, 0, H // 2)
+        load_we(1, 1, H // 2, H)
+        nc.sync.dma_start(out=wt_w[:], in_=words_of(wt_words, 0))
+
+        def gather(dst, window, dtype, offsets, j0, j1):
+            entries = offsets[:, j0 // 16 : j1 // 16]
+            nc.vector.tensor_copy(dst[:, j0:j1], window[:].bitcast(dtype).indirect(entries))
+
+        def permute(w):
+            nc.vector.tensor_copy(
+                out=wf_words[w][:].bitcast(U16).rearrange("p (t m) -> p t m", t=PACK),
+                in_=wf_words_raw[w][:].bitcast(U16).rearrange("p (m t) -> p t m", t=PACK),
+            )
+            nc.vector.tensor_copy(
+                out=wf_scales[w][:].rearrange("p (t m) -> p t m", t=PACK),
+                in_=wf_scales_raw[w][:].bitcast(U8).rearrange("p (m t) -> p t m", t=PACK),
+            )
+
+        def cast(w, a, m0, m1):
+            nc.scalar.activation(
+                out=we_bf[w][a][:].rearrange("p (t m j) -> p m j t", t=PACK, j=PACK)[:, m0:m1],
+                in_=we_raw[w][a][:].rearrange("p j (m t) -> p m j t", t=PACK)[:, m0:m1],
+                func=ACT.Copy,
+            )
+
+        def quantize_we(w, a):
+            nc.vector.quantize_mx(out=we_words[w][a][:].bitcast(FP8X4), scales=we_scales[w][a][:], in_=we_bf[w][a][:])
+
+        def interleaved(bank):
+            return bank[:].rearrange("p t n -> p n t")
+
+        def as_nt(tile):
+            return tile[:].rearrange("p (n t) -> p n t", t=PACK)
+
+        def field(w, c):
+            cols = slice(C * c, C * (c + 1))
+            bank = banks[F_BANKS[w][c]]
+            for t in range(PACK):
+                nc.tensor.matmul_mx(
+                    out=bank[:, t, :],
+                    lhsT=wf_words[w][:, 2 * P * t : 2 * P * (t + 1)].bitcast(FP4X4),
+                    lhsT_scale=wf_scales[w][:, P * t : P * (t + 1)],
+                    rhs=gv2_words[:, cols].bitcast(FP8X4),
+                    rhs_scale=gv2_scales[:, cols],
+                    start=True, stop=True,
+                )
+            nc.scalar.activation(out=as_nt(f_sb[w][c]), in_=interleaved(bank), func=ACT.Copy)
+
+        def edge(w, c):
+            cols = slice(C * c, C * (c + 1))
+            bank = banks[E_BANKS[w][c]]
+            for t in range(PACK):
+                for a in range(2):
+                    nc.tensor.matmul_mx(
+                        out=bank[:, t, :],
+                        lhsT=we_words[w][a][:, P * t : P * (t + 1)].bitcast(FP8X4),
+                        lhsT_scale=we_scales[w][a][:, P * t : P * (t + 1)],
+                        rhs=gv_words[a][:, cols].bitcast(FP8X4),
+                        rhs_scale=gv_scales[4 * a : P, cols],
+                        start=(a == 0), stop=(a == 1),
+                    )
+            nc.vector.tensor_tensor(out=prod[w][:, PACK * C * c : PACK * C * (c + 1)].rearrange("p (n t) -> p n t", t=PACK), in0=interleaved(bank), in1=as_nt(f_sb[1 - w][c]), op=ALU.mult)
+
+        def difference(c0, c1):
+            cols = slice(PACK * C * c0, PACK * C * c1)
+            nc.vector.tensor_tensor(out=h_bf[:, cols], in0=prod[0][:, cols], in1=prod[1][:, cols], op=ALU.subtract)
+
+        def quantize_h(c0, c1):
+            nc.vector.quantize_mx(
+                out=h_words[:, C * c0 : C * c1].bitcast(FP8X4),
+                scales=h_scales[:, C * c0 : C * c1],
+                in_=h_bf[:, PACK * C * c0 : PACK * C * c1],
+            )
+
+        def torque(c):
+            bank = banks[Y_BANKS[c]]
+            for u in range(NT):
+                nc.tensor.matmul_mx(
+                    out=bank[:, u, :],
+                    lhsT=wt_w[:, P * u : P * (u + 1)].bitcast(FP8X4),
+                    lhsT_scale=wt_s[:].bitcast(U8)[:, P * u : P * (u + 1)],
+                    rhs=h_words[:, C * c : C * (c + 1)].bitcast(FP8X4),
+                    rhs_scale=h_scales[:, C * c : C * (c + 1)],
+                    start=True, stop=True,
+                )
+            for u in range(NT):
+                nc.scalar.activation(
+                    out=y_sb[:, u, C * c : C * (c + 1)], in_=bank[:, u, :],
+                    func=ACT.Identity, bias=neg_tl[:, u : u + 1], scale=1.0,
+                )
+            for c0, c1 in STORE_GROUPS:
+                if c1 == c + 1:
+                    nc.sync.dma_start(
+                        out=out.rearrange("(u p) n -> p u n", p=P)[:, :, C * c0 : C * c1],
+                        in_=y_sb[:, :, C * c0 : C * c1],
+                    )
+
+        gather(gv2_scales, v2_scales, U8, idx2, 0, S)
+        gather(gv2_words, v2_words, U32, idx2, 0, HALF)
+        permute(1)
+        gather(gv2_words, v2_words, U32, idx2, HALF, S)
+        gather(gv_words[0], v_words[0], U32, idx, 0, S)
+        cast(0, 0, 0, P)
+        cast(0, 1, 0, P // 2)
+        cast(0, 1, P // 2, P)
+        for c in range(CHUNKS):
+            field(1, c)
+        gather(gv_scales, v_scales, U8, idx, 0, S)
+        permute(0)
+        quantize_we(0, 0)
+        quantize_we(0, 1)
+        cast(1, 0, 0, P)
+        cast(1, 1, 0, P // 2)
+        cast(1, 1, P // 2, P)
+        for c in range(5):
+            field(0, c)
+        nc.scalar.activation(out=neg_tl[:], in_=tl_col[:], func=ACT.Copy, scale=-1.0)
+        gather(gv_words[1], v_words[1], U32, idx, 0, HALF)
+        gather(gv_words[1], v_words[1], U32, idx, HALF, S)
+        quantize_we(1, 0)
+        quantize_we(1, 1)
+        for c in range(CHUNKS):
+            edge(0, c)
+            if c >= 5:
+                field(0, c)
+        groups = STORE_GROUPS
+        for step in range(len(groups) + 1):
+            chunks = list(range(*groups[step])) if step < len(groups) else []
+            if chunks:
+                edge(1, chunks[0])
+            if step >= 1:
+                difference(*groups[step - 1])
+            for c in chunks[1:]:
+                edge(1, c)
+            if step >= 1:
+                quantize_h(*groups[step - 1])
+                for c in range(*groups[step - 1]):
+                    torque(c)

@@ -24,8 +24,10 @@ HALF = S // 2
 NT = N // P
 F_BANKS = ((0, 1, 2, 3, 4, 0, 1, 2), (0, 1, 2, 3, 4, 5, 6, 7))
 E_BANKS = ((5, 6, 7, 0, 1, 2, 3, 4), (5, 6, 7, 3, 5, 6, 7, 3))
-Y_BANKS = (4, 0, 1, 2, 4, 0, 1, 2)
-STORE_GROUPS = ((0, 2), (2, 4), (4, 6), (6, 7), (7, 8))
+Y_BANKS = ((4, 0), (1, 2), (4, 0), (1,), (2,))
+GROUPS = ((0, 256), (256, 256), (512, 256), (768, 128), (896, 128))
+GP_TOKENS = (104, 104, 104, 0, 0)
+UNITS = [(j0, width, t0) for j0, width in GROUPS for t0 in range(0, PACK, 512 // width)]
 
 
 def tile_list_edge_field_torque_kernel(
@@ -36,7 +38,7 @@ def tile_list_edge_field_torque_kernel(
     with ExitStack() as ctx:
         keep = ctx.enter_context(tc.tile_pool(name="keep", bufs=1))
         psum = ctx.enter_context(tc.psum_pool(name="psum", bufs=1))
-        banks = [psum.tile([P, PACK, C], F32, name="bank%d" % b) for b in range(8)]
+        banks = [psum.tile([P, 512], F32, name="bank%d" % b) for b in range(8)]
 
         def sb(name, shape, dtype):
             return keep.tile(shape, dtype, name=name, align_bytes=64)
@@ -65,7 +67,7 @@ def tile_list_edge_field_torque_kernel(
         neg_tl = sb("neg_tl", [P, NT], F32)
         f_sb = [[sb("f_sb%d%d" % (w, c), [P, C * PACK], F32) for c in range(CHUNKS)] for w in range(2)]
         prod = [sb("prod%d" % w, [P, S * PACK], F32) for w in range(2)]
-        h_bf = sb("h_bf", [P, S * PACK], BF16)
+        h_bf = [sb("h_bf%d" % b, [P, 256 * PACK], BF16) for b in range(2)]
         h_words = sb("h_words", [P, S], U32)
         h_scales = sb("h_scales", [P, S], U8)
         y_sb = sb("y_sb", [P, NT, S], F32)
@@ -73,155 +75,164 @@ def tile_list_edge_field_torque_kernel(
         def words_of(dram, a):
             return dram[a].rearrange("p t i -> p (t i)").bitcast(I32)
 
-        def load_scale_rows(engine, tile, dram, a):
+        def load_scale_rows(tile, dram, a):
             for q in range(4):
                 first = 32 * q + 4 * a
-                engine.dma_start(out=tile[first : first + 4, :], in_=dram[a, 4 * q : 4 * q + 4, :].bitcast(I32))
+                nc.sync.dma_start(out=tile[first : first + 4, :], in_=dram[a, 4 * q : 4 * q + 4, :].bitcast(I32))
 
-        def fill_scale_rows(tile, dram, quadrants):
-            for q in quadrants:
-                nc.sync.dma_start(
-                    out=tile[32 * q : 32 * (q + 1), :],
-                    in_=dram[0, 4 * q : 4 * q + 4, :].bitcast(I32).partition_broadcast(8),
-                )
+        def load_words(tile, dram, a, t0, t1):
+            nc.sync.dma_start(out=tile[:, t0:t1], in_=words_of(dram, a)[:, t0:t1])
 
         def load_we(w, a, c0, c1):
             rows = (wex, wey)[w][512 * a : 512 * (a + 1), c0:c1]
             nc.sync.dma_start(out=we_raw[w][a][:, :, c0:c1], in_=rows.rearrange("(p j) c -> p j c", j=PACK))
 
-        for tile in (wf_scales_raw[1], wf_scales_raw[0], wt_s, v_scales):
+        nc.gpsimd.memset(v2_scales[:], 0)
+        for tile in (wf_scales_raw[1], v_scales, wf_scales_raw[0], wt_s):
             nc.vector.memset(tile[:], 0)
 
-        load_scale_rows(nc.gpsimd, wf_scales_raw[1], wfy_scales, 0)
-        load_scale_rows(nc.gpsimd, wf_scales_raw[0], wfx_scales, 0)
-        load_scale_rows(nc.gpsimd, wt_s, wt_scales, 0)
         nc.sync.dma_start(idx2[:], offs2)
-        fill_scale_rows(v2_scales, tab2_scales, range(4))
         nc.sync.dma_start(out=wf_words_raw[1][:], in_=wfy_words[0].bitcast(I32))
-        nc.sync.dma_start(out=v2_words[:], in_=words_of(tab2_words, 0))
-        nc.sync.dma_start(out=v_words[0][:], in_=words_of(tab_words, 0))
+        load_scale_rows(v2_scales, tab2_scales, 0)
+        load_words(v2_words, tab2_words, 0, 0, T2)
+        load_scale_rows(wf_scales_raw[1], wfy_scales, 0)
+        load_words(v_words[0], tab_words, 0, 0, T // 2)
         nc.sync.dma_start(idx[:], offs)
-        load_scale_rows(nc.sync, v_scales, tab_scales, 0)
-        load_we(0, 0, 0, H)
+        load_scale_rows(v_scales, tab_scales, 0)
+        load_words(v_words[0], tab_words, 0, T // 2, T)
+        load_scale_rows(v_scales, tab_scales, 1)
         nc.sync.dma_start(out=wf_words_raw[0][:], in_=wfx_words[0].bitcast(I32))
-        load_scale_rows(nc.sync, v_scales, tab_scales, 1)
-        nc.sync.dma_start(out=v_words[1][:], in_=words_of(tab_words, 1))
-        load_we(0, 1, 0, H // 2)
-        load_we(0, 1, H // 2, H)
+        load_we(0, 1, 0, H)
+        load_scale_rows(wf_scales_raw[0], wfx_scales, 0)
+        load_words(v_words[1], tab_words, 1, 0, T)
+        load_we(0, 0, 0, H // 2)
+        load_we(0, 0, H // 2, H)
         load_we(1, 0, 0, H)
         with nc.allow_non_contiguous_dma(reason="one value of tl to a partition"):
             nc.sync.dma_start(out=tl_col[:], in_=tl.rearrange("(c p) -> p c", p=P))
         load_we(1, 1, 0, H // 2)
         load_we(1, 1, H // 2, H)
-        nc.sync.dma_start(out=wt_w[:], in_=words_of(wt_words, 0))
+        load_words(wt_w, wt_words, 0, 0, N)
+        load_scale_rows(wt_s, wt_scales, 0)
 
         def gather(dst, window, dtype, offsets, j0, j1):
             entries = offsets[:, j0 // 16 : j1 // 16]
             nc.vector.tensor_copy(dst[:, j0:j1], window[:].bitcast(dtype).indirect(entries))
 
         def permute(w):
-            nc.vector.tensor_copy(
+            nc.gpsimd.tensor_copy(
                 out=wf_words[w][:].bitcast(U16).rearrange("p (t m) -> p t m", t=PACK),
                 in_=wf_words_raw[w][:].bitcast(U16).rearrange("p (m t) -> p t m", t=PACK),
             )
-            nc.vector.tensor_copy(
+            nc.gpsimd.tensor_copy(
                 out=wf_scales[w][:].rearrange("p (t m) -> p t m", t=PACK),
                 in_=wf_scales_raw[w][:].bitcast(U8).rearrange("p (m t) -> p t m", t=PACK),
             )
 
-        def cast(w, a, m0, m1):
-            nc.scalar.activation(
-                out=we_bf[w][a][:].rearrange("p (t m j) -> p m j t", t=PACK, j=PACK)[:, m0:m1],
-                in_=we_raw[w][a][:].rearrange("p j (m t) -> p m j t", t=PACK)[:, m0:m1],
-                func=ACT.Copy,
-            )
+        def cast(w, a, m0, m1, on_vector=False):
+            dst = we_bf[w][a][:].rearrange("p (t m j) -> p m j t", t=PACK, j=PACK)[:, m0:m1]
+            src = we_raw[w][a][:].rearrange("p j (m t) -> p m j t", t=PACK)[:, m0:m1]
+            if on_vector:
+                nc.vector.tensor_copy(out=dst, in_=src)
+            else:
+                nc.scalar.activation(out=dst, in_=src, func=ACT.Copy)
 
         def quantize_we(w, a):
             nc.vector.quantize_mx(out=we_words[w][a][:].bitcast(FP8X4), scales=we_scales[w][a][:], in_=we_bf[w][a][:])
 
-        def interleaved(bank):
-            return bank[:].rearrange("p t n -> p n t")
+        def interleaved(bank, width):
+            return bank[:].rearrange("p (t n) -> p n t", n=width)
 
-        def as_nt(tile):
-            return tile[:].rearrange("p (n t) -> p n t", t=PACK)
+        def as_nt(ap, width):
+            return ap.rearrange("p (n t) -> p n t", n=width)
 
         def field(w, c):
-            cols = slice(C * c, C * (c + 1))
+            j0, width, t0 = UNITS[c]
+            cols = slice(j0, j0 + width)
             bank = banks[F_BANKS[w][c]]
-            for t in range(PACK):
+            for i in range(512 // width):
+                t = t0 + i
                 nc.tensor.matmul_mx(
-                    out=bank[:, t, :],
+                    out=bank[:, width * i : width * (i + 1)],
                     lhsT=wf_words[w][:, 2 * P * t : 2 * P * (t + 1)].bitcast(FP4X4),
                     lhsT_scale=wf_scales[w][:, P * t : P * (t + 1)],
                     rhs=gv2_words[:, cols].bitcast(FP8X4),
                     rhs_scale=gv2_scales[:, cols],
                     start=True, stop=True,
                 )
-            nc.scalar.activation(out=as_nt(f_sb[w][c]), in_=interleaved(bank), func=ACT.Copy)
+            nc.scalar.activation(out=as_nt(f_sb[w][c][:], width), in_=interleaved(bank, width), func=ACT.Copy)
 
         def edge(w, c):
-            cols = slice(C * c, C * (c + 1))
+            j0, width, t0 = UNITS[c]
+            cols = slice(j0, j0 + width)
             bank = banks[E_BANKS[w][c]]
-            for t in range(PACK):
-                for a in range(2):
+            passes = ((1, 0), (0, 1))[w]
+            for i in range(512 // width):
+                t = t0 + i
+                for a in passes:
                     nc.tensor.matmul_mx(
-                        out=bank[:, t, :],
+                        out=bank[:, width * i : width * (i + 1)],
                         lhsT=we_words[w][a][:, P * t : P * (t + 1)].bitcast(FP8X4),
                         lhsT_scale=we_scales[w][a][:, P * t : P * (t + 1)],
                         rhs=gv_words[a][:, cols].bitcast(FP8X4),
                         rhs_scale=gv_scales[4 * a : P, cols],
-                        start=(a == 0), stop=(a == 1),
+                        start=(a == passes[0]), stop=(a == passes[1]),
                     )
-            nc.vector.tensor_tensor(out=prod[w][:, PACK * C * c : PACK * C * (c + 1)].rearrange("p (n t) -> p n t", t=PACK), in0=interleaved(bank), in1=as_nt(f_sb[1 - w][c]), op=ALU.mult)
-
-        def difference(c0, c1):
-            cols = slice(PACK * C * c0, PACK * C * c1)
-            nc.vector.tensor_tensor(out=h_bf[:, cols], in0=prod[0][:, cols], in1=prod[1][:, cols], op=ALU.subtract)
-
-        def quantize_h(c0, c1):
-            nc.vector.quantize_mx(
-                out=h_words[:, C * c0 : C * c1].bitcast(FP8X4),
-                scales=h_scales[:, C * c0 : C * c1],
-                in_=h_bf[:, PACK * C * c0 : PACK * C * c1],
+            nc.vector.tensor_tensor(
+                out=as_nt(prod[w][:, 512 * c : 512 * (c + 1)], width),
+                in0=interleaved(bank, width), in1=as_nt(f_sb[1 - w][c][:], width), op=ALU.mult,
             )
 
-        def torque(c):
-            bank = banks[Y_BANKS[c]]
+        def difference(engine, g, n0, n1):
+            j0, width = GROUPS[g]
+            cols = slice(PACK * j0, PACK * (j0 + width))
+            units = width // P
+            ins = [prod[w][:, cols].rearrange("p (u n t) -> p n u t", u=units, n=width)[:, n0:n1] for w in range(2)]
+            engine.tensor_tensor(
+                out=h_bf[g % 2][:, : PACK * width].rearrange("p (n u t) -> p n u t", u=units, n=width)[:, n0:n1],
+                in0=ins[0], in1=ins[1], op=ALU.subtract,
+            )
+
+        def torque(g):
+            j0, width = GROUPS[g]
+            cols = slice(j0, j0 + width)
+            nc.vector.quantize_mx(
+                out=h_words[:, cols].bitcast(FP8X4), scales=h_scales[:, cols],
+                in_=h_bf[g % 2][:, : PACK * width],
+            )
+            sums = []
             for u in range(NT):
+                b, first = divmod(width * u, 512)
+                sums.append(banks[Y_BANKS[g][b]][:, first : first + width])
                 nc.tensor.matmul_mx(
-                    out=bank[:, u, :],
+                    out=sums[u],
                     lhsT=wt_w[:, P * u : P * (u + 1)].bitcast(FP8X4),
                     lhsT_scale=wt_s[:].bitcast(U8)[:, P * u : P * (u + 1)],
-                    rhs=h_words[:, C * c : C * (c + 1)].bitcast(FP8X4),
-                    rhs_scale=h_scales[:, C * c : C * (c + 1)],
+                    rhs=h_words[:, cols].bitcast(FP8X4),
+                    rhs_scale=h_scales[:, cols],
                     start=True, stop=True,
                 )
             for u in range(NT):
                 nc.scalar.activation(
-                    out=y_sb[:, u, C * c : C * (c + 1)], in_=bank[:, u, :],
-                    func=ACT.Identity, bias=neg_tl[:, u : u + 1], scale=1.0,
+                    out=y_sb[:, u, cols], in_=sums[u], func=ACT.Identity, bias=neg_tl[:, u : u + 1], scale=1.0,
                 )
-            for c0, c1 in STORE_GROUPS:
-                if c1 == c + 1:
-                    nc.sync.dma_start(
-                        out=out.rearrange("(u p) n -> p u n", p=P)[:, :, C * c0 : C * c1],
-                        in_=y_sb[:, :, C * c0 : C * c1],
-                    )
+            nc.sync.dma_start(out=out.rearrange("(u p) n -> p u n", p=P)[:, :, cols], in_=y_sb[:, :, cols])
 
         gather(gv2_scales, v2_scales, U8, idx2, 0, S)
         gather(gv2_words, v2_words, U32, idx2, 0, HALF)
         permute(1)
         gather(gv2_words, v2_words, U32, idx2, HALF, S)
         gather(gv_words[0], v_words[0], U32, idx, 0, S)
-        cast(0, 0, 0, P)
-        cast(0, 1, 0, P // 2)
-        cast(0, 1, P // 2, P)
+        cast(0, 1, 0, P)
+        cast(0, 0, 0, P // 2)
+        cast(0, 0, P // 2, 3 * P // 4)
         for c in range(CHUNKS):
             field(1, c)
         gather(gv_scales, v_scales, U8, idx, 0, S)
         permute(0)
-        quantize_we(0, 0)
         quantize_we(0, 1)
+        cast(0, 0, 3 * P // 4, P, True)
+        quantize_we(0, 0)
         cast(1, 0, 0, P)
         cast(1, 1, 0, P // 2)
         cast(1, 1, P // 2, P)
@@ -236,16 +247,30 @@ def tile_list_edge_field_torque_kernel(
             edge(0, c)
             if c >= 5:
                 field(0, c)
-        groups = STORE_GROUPS
-        for step in range(len(groups) + 1):
-            chunks = list(range(*groups[step])) if step < len(groups) else []
-            if chunks:
-                edge(1, chunks[0])
-            if step >= 1:
-                difference(*groups[step - 1])
-            for c in chunks[1:]:
-                edge(1, c)
-            if step >= 1:
-                quantize_h(*groups[step - 1])
-                for c in range(*groups[step - 1]):
-                    torque(c)
+        def diff_vector(g):
+            difference(nc.vector, g, GP_TOKENS[g], GROUPS[g][1])
+
+        def diff_gpsimd(g):
+            difference(nc.gpsimd, g, 0, GP_TOKENS[g])
+
+        edge(1, 0)
+        edge(1, 1)
+        diff_gpsimd(0)
+        edge(1, 2)
+        edge(1, 3)
+        diff_vector(0)
+        diff_gpsimd(1)
+        edge(1, 4)
+        edge(1, 5)
+        torque(0)
+        diff_vector(1)
+        diff_gpsimd(2)
+        edge(1, 6)
+        edge(1, 7)
+        torque(1)
+        diff_vector(2)
+        diff_vector(3)
+        torque(2)
+        diff_vector(4)
+        torque(3)
+        torque(4)

@@ -26,7 +26,7 @@ F_BANKS = ((0, 1, 2, 3, 4, 0, 1, 2), (0, 1, 2, 3, 4, 5, 6, 7))
 E_BANKS = ((5, 6, 7, 0, 1, 2, 3, 4), (5, 6, 7, 3, 5, 6, 7, 3))
 Y_BANKS = ((4, 0), (1, 2), (4, 0), (1,), (2,))
 GROUPS = ((0, 256), (256, 256), (512, 256), (768, 128), (896, 128))
-GP_TOKENS = (104, 104, 104, 0, 0)
+GP_TOKENS = (0, 0, 0, 0, 0)
 UNITS = [(j0, width, t0) for j0, width in GROUPS for t0 in range(0, PACK, 512 // width)]
 
 
@@ -75,10 +75,10 @@ def tile_list_edge_field_torque_kernel(
         def words_of(dram, a):
             return dram[a].rearrange("p t i -> p (t i)").bitcast(I32)
 
-        def load_scale_rows(tile, dram, a):
-            for q in range(4):
-                first = 32 * q + 4 * a
-                nc.sync.dma_start(out=tile[first : first + 4, :], in_=dram[a, 4 * q : 4 * q + 4, :].bitcast(I32))
+        def load_scale_rows(tile, dram, rows=range(4)):
+            for r in rows:
+                for a in range(dram.shape[0]):
+                    nc.sync.dma_start(out=tile[4 * a + r : P : 32, :], in_=dram[a, r:16:4, :].bitcast(I32))
 
         def load_words(tile, dram, a, t0, t1):
             nc.sync.dma_start(out=tile[:, t0:t1], in_=words_of(dram, a)[:, t0:t1])
@@ -93,38 +93,38 @@ def tile_list_edge_field_torque_kernel(
 
         nc.sync.dma_start(idx2[:], offs2)
         nc.sync.dma_start(out=wf_words_raw[1][:], in_=wfy_words[0].bitcast(I32))
-        load_scale_rows(v2_scales, tab2_scales, 0)
+        load_scale_rows(v2_scales, tab2_scales)
         load_words(v2_words, tab2_words, 0, 0, T2)
-        load_scale_rows(wf_scales_raw[1], wfy_scales, 0)
+        load_scale_rows(wf_scales_raw[1], wfy_scales)
         load_words(v_words[0], tab_words, 0, 0, T // 2)
         nc.sync.dma_start(idx[:], offs)
-        load_scale_rows(v_scales, tab_scales, 0)
+        load_scale_rows(v_scales, tab_scales, range(0, 2))
         load_words(v_words[0], tab_words, 0, T // 2, T)
-        load_scale_rows(v_scales, tab_scales, 1)
+        load_scale_rows(v_scales, tab_scales, range(2, 4))
         nc.sync.dma_start(out=wf_words_raw[0][:], in_=wfx_words[0].bitcast(I32))
         load_we(0, 1, 0, H)
-        load_scale_rows(wf_scales_raw[0], wfx_scales, 0)
+        load_scale_rows(wf_scales_raw[0], wfx_scales)
         load_words(v_words[1], tab_words, 1, 0, T)
         load_we(0, 0, 0, H // 2)
         load_we(0, 0, H // 2, H)
         load_we(1, 0, 0, H)
-        with nc.allow_non_contiguous_dma(reason="one value of tl to a partition"):
-            nc.sync.dma_start(out=tl_col[:], in_=tl.rearrange("(c p) -> p c", p=P))
         load_we(1, 1, 0, H // 2)
         load_we(1, 1, H // 2, H)
         load_words(wt_w, wt_words, 0, 0, N)
-        load_scale_rows(wt_s, wt_scales, 0)
+        load_scale_rows(wt_s, wt_scales)
+        with nc.allow_non_contiguous_dma(reason="one value of tl to a partition"):
+            nc.sync.dma_start(out=tl_col[:], in_=tl.rearrange("(c p) -> p c", p=P))
 
         def gather(dst, window, dtype, offsets, j0, j1):
             entries = offsets[:, j0 // 16 : j1 // 16]
             nc.vector.tensor_copy(dst[:, j0:j1], window[:].bitcast(dtype).indirect(entries))
 
         def permute(w):
-            nc.gpsimd.tensor_copy(
+            nc.vector.tensor_copy(
                 out=wf_words[w][:].bitcast(U16).rearrange("p (t m) -> p t m", t=PACK),
                 in_=wf_words_raw[w][:].bitcast(U16).rearrange("p (m t) -> p t m", t=PACK),
             )
-            nc.gpsimd.tensor_copy(
+            nc.vector.tensor_copy(
                 out=wf_scales[w][:].rearrange("p (t m) -> p t m", t=PACK),
                 in_=wf_scales_raw[w][:].bitcast(U8).rearrange("p (m t) -> p t m", t=PACK),
             )
@@ -238,7 +238,6 @@ def tile_list_edge_field_torque_kernel(
         cast(1, 1, P // 2, P)
         for c in range(5):
             field(0, c)
-        nc.scalar.activation(out=neg_tl[:], in_=tl_col[:], func=ACT.Copy, scale=-1.0)
         gather(gv_words[1], v_words[1], U32, idx, 0, HALF)
         gather(gv_words[1], v_words[1], U32, idx, HALF, S)
         quantize_we(1, 0)
@@ -247,6 +246,8 @@ def tile_list_edge_field_torque_kernel(
             edge(0, c)
             if c >= 5:
                 field(0, c)
+        nc.scalar.activation(out=neg_tl[:], in_=tl_col[:], func=ACT.Copy, scale=-1.0)
+
         def diff_vector(g):
             difference(nc.vector, g, GP_TOKENS[g], GROUPS[g][1])
 
@@ -255,20 +256,17 @@ def tile_list_edge_field_torque_kernel(
 
         edge(1, 0)
         edge(1, 1)
-        diff_gpsimd(0)
         edge(1, 2)
-        edge(1, 3)
         diff_vector(0)
-        diff_gpsimd(1)
-        edge(1, 4)
-        edge(1, 5)
+        edge(1, 3)
         torque(0)
+        edge(1, 4)
         diff_vector(1)
-        diff_gpsimd(2)
-        edge(1, 6)
-        edge(1, 7)
+        edge(1, 5)
         torque(1)
+        edge(1, 6)
         diff_vector(2)
+        edge(1, 7)
         diff_vector(3)
         torque(2)
         diff_vector(4)

@@ -22,11 +22,14 @@ C = 128
 CHUNKS = S // C
 HALF = S // 2
 NT = N // P
-F_BANKS = ((0, 1, 2, 3, 4, 0, 1, 2), (0, 1, 2, 3, 4, 5, 6, 7))
-E_BANKS = ((5, 6, 7, 0, 1, 2, 3, 4), (5, 6, 7, 3, 5, 6, 7, 3))
-Y_BANKS = ((4, 0), (1, 2), (4, 0), (1,), (2,))
+F_BANKS = ((0, 1, 2, 3, 4, 5, 0, 1), (0, 1, 2, 3, 4, 5, 6, 7))
+E_BANKS = ((6, 7, 0, 1, 2, 3, 4, 5), (6, 7, 2, 3, 4, 5, 6, 7))
+Y_BANKS = ((0, 1), (2, 3), (4, 5), (0,), (1,))
 GROUPS = ((0, 256), (256, 256), (512, 256), (768, 128), (896, 128))
-GP_TOKENS = (0, 0, 0, 0, 0)
+GP_TOKENS = (80, 104, 104, 0, 0)
+VECTOR_OUT = ((4, 0), (4, 1), (4, 2))
+H_BUFS = (0, 1, 0, 2, 1)
+STORE_BY_TILE = (2,)
 UNITS = [(j0, width, t0) for j0, width in GROUPS for t0 in range(0, PACK, 512 // width)]
 
 
@@ -67,7 +70,7 @@ def tile_list_edge_field_torque_kernel(
         neg_tl = sb("neg_tl", [P, NT], F32)
         f_sb = [[sb("f_sb%d%d" % (w, c), [P, C * PACK], F32) for c in range(CHUNKS)] for w in range(2)]
         prod = [sb("prod%d" % w, [P, S * PACK], F32) for w in range(2)]
-        h_bf = [sb("h_bf%d" % b, [P, 256 * PACK], BF16) for b in range(2)]
+        h_bf = [sb("h_bf%d" % b, [P, 256 * PACK], BF16) for b in range(3)]
         h_words = sb("h_words", [P, S], U32)
         h_scales = sb("h_scales", [P, S], U8)
         y_sb = sb("y_sb", [P, NT, S], F32)
@@ -102,29 +105,31 @@ def tile_list_edge_field_torque_kernel(
         load_words(v_words[0], tab_words, 0, T // 2, T)
         load_scale_rows(v_scales, tab_scales, range(2, 4))
         nc.sync.dma_start(out=wf_words_raw[0][:], in_=wfx_words[0].bitcast(I32))
+        load_scale_rows(wf_scales_raw[0], wfx_scales, range(0, 1))
         load_we(0, 1, 0, H)
-        load_scale_rows(wf_scales_raw[0], wfx_scales)
+        load_scale_rows(wf_scales_raw[0], wfx_scales, range(1, 4))
         load_words(v_words[1], tab_words, 1, 0, T)
         load_we(0, 0, 0, H // 2)
         load_we(0, 0, H // 2, H)
-        load_we(1, 0, 0, H)
+        load_we(1, 0, 0, H // 2)
+        load_we(1, 0, H // 2, H)
         load_we(1, 1, 0, H // 2)
         load_we(1, 1, H // 2, H)
-        load_words(wt_w, wt_words, 0, 0, N)
-        load_scale_rows(wt_s, wt_scales)
         with nc.allow_non_contiguous_dma(reason="one value of tl to a partition"):
             nc.sync.dma_start(out=tl_col[:], in_=tl.rearrange("(c p) -> p c", p=P))
+        load_words(wt_w, wt_words, 0, 0, N)
+        load_scale_rows(wt_s, wt_scales)
 
         def gather(dst, window, dtype, offsets, j0, j1):
             entries = offsets[:, j0 // 16 : j1 // 16]
             nc.vector.tensor_copy(dst[:, j0:j1], window[:].bitcast(dtype).indirect(entries))
 
         def permute(w):
-            nc.vector.tensor_copy(
+            nc.gpsimd.tensor_copy(
                 out=wf_words[w][:].bitcast(U16).rearrange("p (t m) -> p t m", t=PACK),
                 in_=wf_words_raw[w][:].bitcast(U16).rearrange("p (m t) -> p t m", t=PACK),
             )
-            nc.vector.tensor_copy(
+            nc.gpsimd.tensor_copy(
                 out=wf_scales[w][:].rearrange("p (t m) -> p t m", t=PACK),
                 in_=wf_scales_raw[w][:].bitcast(U8).rearrange("p (m t) -> p t m", t=PACK),
             )
@@ -137,8 +142,11 @@ def tile_list_edge_field_torque_kernel(
             else:
                 nc.scalar.activation(out=dst, in_=src, func=ACT.Copy)
 
-        def quantize_we(w, a):
-            nc.vector.quantize_mx(out=we_words[w][a][:].bitcast(FP8X4), scales=we_scales[w][a][:], in_=we_bf[w][a][:])
+        def quantize_we(w, a, c0=0, c1=H):
+            nc.vector.quantize_mx(
+                out=we_words[w][a][:, c0:c1].bitcast(FP8X4), scales=we_scales[w][a][:, c0:c1],
+                in_=we_bf[w][a][:, PACK * c0 : PACK * c1],
+            )
 
         def interleaved(bank, width):
             return bank[:].rearrange("p (t n) -> p n t", n=width)
@@ -189,7 +197,7 @@ def tile_list_edge_field_torque_kernel(
             units = width // P
             ins = [prod[w][:, cols].rearrange("p (u n t) -> p n u t", u=units, n=width)[:, n0:n1] for w in range(2)]
             engine.tensor_tensor(
-                out=h_bf[g % 2][:, : PACK * width].rearrange("p (n u t) -> p n u t", u=units, n=width)[:, n0:n1],
+                out=h_bf[H_BUFS[g]][:, : PACK * width].rearrange("p (n u t) -> p n u t", u=units, n=width)[:, n0:n1],
                 in0=ins[0], in1=ins[1], op=ALU.subtract,
             )
 
@@ -198,7 +206,7 @@ def tile_list_edge_field_torque_kernel(
             cols = slice(j0, j0 + width)
             nc.vector.quantize_mx(
                 out=h_words[:, cols].bitcast(FP8X4), scales=h_scales[:, cols],
-                in_=h_bf[g % 2][:, : PACK * width],
+                in_=h_bf[H_BUFS[g]][:, : PACK * width],
             )
             sums = []
             for u in range(NT):
@@ -213,10 +221,24 @@ def tile_list_edge_field_torque_kernel(
                     start=True, stop=True,
                 )
             for u in range(NT):
-                nc.scalar.activation(
-                    out=y_sb[:, u, cols], in_=sums[u], func=ACT.Identity, bias=neg_tl[:, u : u + 1], scale=1.0,
-                )
-            nc.sync.dma_start(out=out.rearrange("(u p) n -> p u n", p=P)[:, :, cols], in_=y_sb[:, :, cols])
+                if (g, u) in VECTOR_OUT:
+                    nc.vector.tensor_scalar(
+                        out=y_sb[:, u, cols], in0=sums[u], scalar1=tl_col[:, u : u + 1], scalar2=None, op0=ALU.subtract,
+                    )
+                else:
+                    nc.scalar.activation(
+                        out=y_sb[:, u, cols], in_=sums[u], func=ACT.Identity, bias=neg_tl[:, u : u + 1], scale=1.0,
+                    )
+                if g in STORE_BY_TILE:
+                    nc.sync.dma_start(out=out[P * u : P * (u + 1), cols], in_=y_sb[:, u, cols])
+            if g not in STORE_BY_TILE:
+                nc.sync.dma_start(out=out.rearrange("(u p) n -> p u n", p=P)[:, :, cols], in_=y_sb[:, :, cols])
+
+        def diff_vector(g):
+            difference(nc.vector, g, GP_TOKENS[g], GROUPS[g][1])
+
+        def diff_gpsimd(g):
+            difference(nc.gpsimd, g, 0, GP_TOKENS[g])
 
         gather(gv2_scales, v2_scales, U8, idx2, 0, S)
         gather(gv2_words, v2_words, U32, idx2, 0, HALF)
@@ -225,50 +247,66 @@ def tile_list_edge_field_torque_kernel(
         gather(gv_words[0], v_words[0], U32, idx, 0, S)
         cast(0, 1, 0, P)
         cast(0, 0, 0, P // 2)
-        cast(0, 0, P // 2, 3 * P // 4)
-        for c in range(CHUNKS):
-            field(1, c)
+        cast(0, 0, P // 2, 5 * P // 8)
+        cast(0, 0, 5 * P // 8, P, True)
+        field(1, 0)
+        field(1, 1)
+        field(1, 2)
+        field(1, 3)
+        field(1, 4)
+        field(1, 5)
+        field(1, 6)
+        field(1, 7)
         gather(gv_scales, v_scales, U8, idx, 0, S)
         permute(0)
         quantize_we(0, 1)
-        cast(0, 0, 3 * P // 4, P, True)
-        quantize_we(0, 0)
-        cast(1, 0, 0, P)
+        quantize_we(0, 0, 0, H // 2)
+        quantize_we(0, 0, H // 2, H)
+        cast(1, 0, 0, P // 2)
+        cast(1, 0, P // 2, P)
         cast(1, 1, 0, P // 2)
-        cast(1, 1, P // 2, P)
-        for c in range(5):
-            field(0, c)
+        cast(1, 1, P // 2, 5 * P // 8)
+        field(0, 0)
+        field(0, 1)
+        field(0, 2)
+        field(0, 3)
+        field(0, 4)
+        field(0, 5)
         gather(gv_words[1], v_words[1], U32, idx, 0, HALF)
         gather(gv_words[1], v_words[1], U32, idx, HALF, S)
         quantize_we(1, 0)
-        quantize_we(1, 1)
-        for c in range(CHUNKS):
-            edge(0, c)
-            if c >= 5:
-                field(0, c)
+        cast(1, 1, 5 * P // 8, P, True)
+        quantize_we(1, 1, 0, H // 2)
+        quantize_we(1, 1, H // 2, H)
+        edge(0, 0)
+        edge(0, 1)
+        edge(0, 2)
+        edge(0, 3)
+        edge(0, 4)
+        edge(0, 5)
+        edge(0, 6)
+        field(0, 6)
+        edge(0, 7)
+        field(0, 7)
         nc.scalar.activation(out=neg_tl[:], in_=tl_col[:], func=ACT.Copy, scale=-1.0)
-
-        def diff_vector(g):
-            difference(nc.vector, g, GP_TOKENS[g], GROUPS[g][1])
-
-        def diff_gpsimd(g):
-            difference(nc.gpsimd, g, 0, GP_TOKENS[g])
-
         edge(1, 0)
         edge(1, 1)
+        diff_gpsimd(0)
         edge(1, 2)
-        diff_vector(0)
         edge(1, 3)
-        torque(0)
+        diff_vector(0)
+        diff_gpsimd(1)
         edge(1, 4)
-        diff_vector(1)
         edge(1, 5)
-        torque(1)
+        torque(0)
+        diff_vector(1)
+        diff_gpsimd(2)
         edge(1, 6)
-        diff_vector(2)
         edge(1, 7)
-        diff_vector(3)
+        torque(1)
+        diff_vector(2)
         torque(2)
+        diff_vector(3)
         diff_vector(4)
         torque(3)
         torque(4)

@@ -134,9 +134,9 @@ def tile_list_edge_field_torque_kernel(
                 in_=wf_scales_raw[w][:].bitcast(U8).rearrange("p (m t) -> p t m", t=PACK),
             )
 
-        def cast(w, a, m0, m1, on_vector=False):
-            dst = we_bf[w][a][:].rearrange("p (t m j) -> p m j t", t=PACK, j=PACK)[:, m0:m1]
-            src = we_raw[w][a][:].rearrange("p j (m t) -> p m j t", t=PACK)[:, m0:m1]
+        def cast(w, a, m0, m1, on_vector=False, t0=0, t1=PACK):
+            dst = we_bf[w][a][:].rearrange("p (t m j) -> p m j t", t=PACK, j=PACK)[:, m0:m1, :, t0:t1]
+            src = we_raw[w][a][:].rearrange("p j (m t) -> p m j t", t=PACK)[:, m0:m1, :, t0:t1]
             if on_vector:
                 nc.vector.tensor_copy(out=dst, in_=src)
             else:
@@ -241,14 +241,15 @@ def tile_list_edge_field_torque_kernel(
             difference(nc.gpsimd, g, 0, GP_TOKENS[g])
 
         gather(gv2_scales, v2_scales, U8, idx2, 0, S)
+        gather(gv_scales, v_scales, U8, idx, 0, S)
         gather(gv2_words, v2_words, U32, idx2, 0, HALF)
         permute(1)
         gather(gv2_words, v2_words, U32, idx2, HALF, S)
         gather(gv_words[0], v_words[0], U32, idx, 0, S)
         cast(0, 1, 0, P)
         cast(0, 0, 0, P // 2)
-        cast(0, 0, P // 2, 5 * P // 8)
-        cast(0, 0, 5 * P // 8, P, True)
+        cast(0, 0, P // 2, P, False, 2, 4)
+        cast(0, 0, P // 2, P, True, 0, 2)
         field(1, 0)
         field(1, 1)
         field(1, 2)
@@ -257,7 +258,6 @@ def tile_list_edge_field_torque_kernel(
         field(1, 5)
         field(1, 6)
         field(1, 7)
-        gather(gv_scales, v_scales, U8, idx, 0, S)
         permute(0)
         quantize_we(0, 1)
         quantize_we(0, 0, 0, H // 2)
@@ -265,7 +265,7 @@ def tile_list_edge_field_torque_kernel(
         cast(1, 0, 0, P // 2)
         cast(1, 0, P // 2, P)
         cast(1, 1, 0, P // 2)
-        cast(1, 1, P // 2, 5 * P // 8)
+        cast(1, 1, P // 2, 3 * P // 4, False, 2, 4)
         field(0, 0)
         field(0, 1)
         field(0, 2)
@@ -275,7 +275,8 @@ def tile_list_edge_field_torque_kernel(
         gather(gv_words[1], v_words[1], U32, idx, 0, HALF)
         gather(gv_words[1], v_words[1], U32, idx, HALF, S)
         quantize_we(1, 0)
-        cast(1, 1, 5 * P // 8, P, True)
+        cast(1, 1, P // 2, P, True, 0, 2)
+        cast(1, 1, 3 * P // 4, P, True, 2, 4)
         quantize_we(1, 1, 0, H // 2)
         quantize_we(1, 1, H // 2, H)
         edge(0, 0)

@@ -19,18 +19,13 @@ ACT = mybir.ActivationFunctionType
 P = 128
 PACK = 4
 C = 128
-CHUNKS = S // C
+UNITS = S // C
 HALF = S // 2
 NT = N // P
-F_BANKS = ((0, 1, 2, 3, 4, 5, 0, 1), (0, 1, 2, 3, 4, 5, 6, 7))
-E_BANKS = ((6, 7, 0, 1, 2, 3, 4, 5), (6, 7, 2, 3, 4, 5, 6, 7))
-Y_BANKS = ((0, 1), (2, 3), (4, 5), (0,), (1,))
-GROUPS = ((0, 256), (256, 256), (512, 256), (768, 128), (896, 128))
-GP_TOKENS = (80, 104, 104, 0, 0)
-VECTOR_OUT = ((4, 0), (4, 1), (4, 2))
-H_BUFS = (0, 1, 0, 2, 1)
-STORE_BY_TILE = (2,)
-UNITS = [(j0, width, t0) for j0, width in GROUPS for t0 in range(0, PACK, 512 // width)]
+X, Y = 0, 1
+GROUPS = ((0, 1), (2, 3), (4, 5), (6,), (7,))
+GPSIMD_UNITS = 3
+FX_BANKS = 4
 
 
 def tile_list_edge_field_torque_kernel(
@@ -54,6 +49,7 @@ def tile_list_edge_field_torque_kernel(
         v2_scales = sb("v2_scales", [P, T2 // 4], I32)
         gv_words = [sb("gv_words%d" % a, [P, S], U32) for a in range(2)]
         gv_scales = sb("gv_scales", [P, S], U8)
+        gv_rows = sb("gv_rows", [P, S], U8)
         gv2_words = sb("gv2_words", [P, S], U32)
         gv2_scales = sb("gv2_scales", [P, S], U8)
         wf_words_raw = [sb("wf_words_raw%d" % w, [P, H // 2], I32) for w in range(2)]
@@ -61,253 +57,227 @@ def tile_list_edge_field_torque_kernel(
         wf_words = [sb("wf_words%d" % w, [P, 2 * H], U8) for w in range(2)]
         wf_scales = [sb("wf_scales%d" % w, [P, H], U8) for w in range(2)]
         we_raw = [[sb("we_raw%d%d" % (w, a), [P, PACK, H], F32) for a in range(2)] for w in range(2)]
-        we_bf = [[sb("we_bf%d%d" % (w, a), [P, PACK * H], BF16) for a in range(2)] for w in range(2)]
-        we_words = [[sb("we_words%d%d" % (w, a), [P, H], U32) for a in range(2)] for w in range(2)]
-        we_scales = [[sb("we_scales%d%d" % (w, a), [P, H], U8) for a in range(2)] for w in range(2)]
+        we_bf = [sb("we_bf%d" % w, [P, 2 * PACK * H], BF16) for w in range(2)]
+        we_words = [sb("we_words%d" % w, [P, 2 * H], U32) for w in range(2)]
+        we_scales = [sb("we_scales%d" % w, [P, 2 * H], U8) for w in range(2)]
         wt_w = sb("wt_w", [P, N], I32)
         wt_s = sb("wt_s", [P, N // 4], I32)
         tl_col = sb("tl_col", [P, NT], F32)
         neg_tl = sb("neg_tl", [P, NT], F32)
-        f_sb = [[sb("f_sb%d%d" % (w, c), [P, C * PACK], F32) for c in range(CHUNKS)] for w in range(2)]
-        prod = [sb("prod%d" % w, [P, S * PACK], F32) for w in range(2)]
-        h_bf = [sb("h_bf%d" % b, [P, 256 * PACK], BF16) for b in range(3)]
-        h_words = sb("h_words", [P, S], U32)
-        h_scales = sb("h_scales", [P, S], U8)
-        y_sb = sb("y_sb", [P, NT, S], F32)
+        f_sb = [[sb("f_sb%d%d" % (w, u), [P, C * PACK], F32) for u in range(UNITS)] for w in range(2)]
+        prod = [[sb("prod%d%d" % (w, u), [P, C * PACK], F32)[:] for u in range(UNITS)] for w in range(2)]
+        for j, u in enumerate(range(5, 7)):
+            prod[X][u] = we_raw[Y][0][:, j, :]
+        for j, u in enumerate(range(7, UNITS)):
+            prod[X][u] = we_raw[Y][1][:, j, :]
+        h_bf = [sb("h_bf%d" % g, [P, len(units) * C * PACK], BF16) for g, units in enumerate(GROUPS)]
+        h_bf[1] = h_bf[0]
+        h_words = [sb("h_words%d" % g, [P, len(units) * C], U32) for g, units in enumerate(GROUPS)]
+        h_scales = [sb("h_scales%d" % g, [P, len(units) * C], U8) for g, units in enumerate(GROUPS)]
+        y_sb = [sb("y_sb%d" % g, [P, NT, len(units) * C], F32) for g, units in enumerate(GROUPS)]
 
         def words_of(dram, a):
             return dram[a].rearrange("p t i -> p (t i)").bitcast(I32)
 
-        def load_scale_rows(tile, dram, rows=range(4)):
+        def load_scale_rows(tile, dram, queue=nc.sync, rows=range(4)):
             for r in rows:
                 for a in range(dram.shape[0]):
-                    nc.sync.dma_start(out=tile[4 * a + r : P : 32, :], in_=dram[a, r:16:4, :].bitcast(I32))
+                    queue.dma_start(out=tile[4 * a + r : P : 32, :], in_=dram[a, r:16:4, :].bitcast(I32))
 
         def load_words(tile, dram, a, t0, t1):
             nc.sync.dma_start(out=tile[:, t0:t1], in_=words_of(dram, a)[:, t0:t1])
 
-        def load_we(w, a, c0, c1):
+        def load_we(w, a, c0=0, c1=H):
             rows = (wex, wey)[w][512 * a : 512 * (a + 1), c0:c1]
             nc.sync.dma_start(out=we_raw[w][a][:, :, c0:c1], in_=rows.rearrange("(p j) c -> p j c", j=PACK))
 
-        nc.gpsimd.memset(v2_scales[:], 0)
-        for tile in (wf_scales_raw[1], v_scales, wf_scales_raw[0], wt_s):
-            nc.vector.memset(tile[:], 0)
+        def load_wf_words(w):
+            nc.sync.dma_start(out=wf_words_raw[w][:], in_=(wfx_words, wfy_words)[w][0].bitcast(I32))
 
+        for tile in (v2_scales[:], v_scales[:], wf_scales_raw[Y][:], wf_scales_raw[X][:], gv_scales[:].bitcast(I32), wt_s[:]):
+            nc.vector.memset(tile, 0)
+
+        def move_scale_rows(a):
+            for r in range(4):
+                first = 64 * a + 4 * r
+                nc.sync.dma_start(
+                    out=gv_scales[4 * a + r : P : 32, :].bitcast(I32), in_=gv_rows[first : first + 49 : 16, :].bitcast(I32),
+                )
+
+        load_wf_words(Y)
+        load_wf_words(X)
         nc.sync.dma_start(idx2[:], offs2)
-        nc.sync.dma_start(out=wf_words_raw[1][:], in_=wfy_words[0].bitcast(I32))
         load_scale_rows(v2_scales, tab2_scales)
-        load_words(v2_words, tab2_words, 0, 0, T2)
-        load_scale_rows(wf_scales_raw[1], wfy_scales)
-        load_words(v_words[0], tab_words, 0, 0, T // 2)
+        load_we(X, 0)
         nc.sync.dma_start(idx[:], offs)
-        load_scale_rows(v_scales, tab_scales, range(0, 2))
+        nc.sync.dma_start(out=v_scales[0:P:4, :], in_=tab_scales.rearrange("a q t -> (a q) t").bitcast(I32))
+        load_words(v2_words, tab2_words, 0, 0, T2)
+        load_scale_rows(wf_scales_raw[Y], wfy_scales)
+        load_we(X, 1)
+        load_scale_rows(wf_scales_raw[X], wfx_scales)
+        load_words(v_words[0], tab_words, 0, 0, T // 2)
+        nc.vector.tensor_copy(gv_rows[:], v_scales[:].bitcast(U8).indirect(idx[:]))
+        move_scale_rows(0)
         load_words(v_words[0], tab_words, 0, T // 2, T)
-        load_scale_rows(v_scales, tab_scales, range(2, 4))
-        nc.sync.dma_start(out=wf_words_raw[0][:], in_=wfx_words[0].bitcast(I32))
-        load_scale_rows(wf_scales_raw[0], wfx_scales, range(0, 1))
-        load_we(0, 1, 0, H)
-        load_scale_rows(wf_scales_raw[0], wfx_scales, range(1, 4))
+        move_scale_rows(1)
         load_words(v_words[1], tab_words, 1, 0, T)
-        load_we(0, 0, 0, H // 2)
-        load_we(0, 0, H // 2, H)
-        load_we(1, 0, 0, H // 2)
-        load_we(1, 0, H // 2, H)
-        load_we(1, 1, 0, H // 2)
-        load_we(1, 1, H // 2, H)
-        with nc.allow_non_contiguous_dma(reason="one value of tl to a partition"):
-            nc.sync.dma_start(out=tl_col[:], in_=tl.rearrange("(c p) -> p c", p=P))
+        load_we(Y, 0)
+        load_we(Y, 1)
         load_words(wt_w, wt_words, 0, 0, N)
         load_scale_rows(wt_s, wt_scales)
+        with nc.allow_non_contiguous_dma(reason="one value of tl to a partition"):
+            nc.sync.dma_start(out=tl_col[:], in_=tl.rearrange("(c p) -> p c", p=P))
 
         def gather(dst, window, dtype, offsets, j0, j1):
             entries = offsets[:, j0 // 16 : j1 // 16]
             nc.vector.tensor_copy(dst[:, j0:j1], window[:].bitcast(dtype).indirect(entries))
 
-        def permute(w):
-            nc.gpsimd.tensor_copy(
+        def permute_words(w, engine=nc.vector):
+            engine.tensor_copy(
                 out=wf_words[w][:].bitcast(U16).rearrange("p (t m) -> p t m", t=PACK),
                 in_=wf_words_raw[w][:].bitcast(U16).rearrange("p (m t) -> p t m", t=PACK),
             )
-            nc.gpsimd.tensor_copy(
+
+        def permute_scales(w, engine=nc.vector):
+            engine.tensor_copy(
                 out=wf_scales[w][:].rearrange("p (t m) -> p t m", t=PACK),
                 in_=wf_scales_raw[w][:].bitcast(U8).rearrange("p (m t) -> p t m", t=PACK),
             )
 
-        def cast(w, a, m0, m1, on_vector=False, t0=0, t1=PACK):
-            dst = we_bf[w][a][:].rearrange("p (t m j) -> p m j t", t=PACK, j=PACK)[:, m0:m1, :, t0:t1]
+        def cast(w, a, on_vector=False, m0=0, m1=P, t0=0, t1=PACK):
+            dst = we_bf[w][:, PACK * H * a : PACK * H * (a + 1)].rearrange("p (t m j) -> p m j t", t=PACK, j=PACK)[:, m0:m1, :, t0:t1]
             src = we_raw[w][a][:].rearrange("p j (m t) -> p m j t", t=PACK)[:, m0:m1, :, t0:t1]
             if on_vector:
                 nc.vector.tensor_copy(out=dst, in_=src)
             else:
                 nc.scalar.activation(out=dst, in_=src, func=ACT.Copy)
 
-        def quantize_we(w, a, c0=0, c1=H):
+        def quantize_we(w, c0, c1):
             nc.vector.quantize_mx(
-                out=we_words[w][a][:, c0:c1].bitcast(FP8X4), scales=we_scales[w][a][:, c0:c1],
-                in_=we_bf[w][a][:, PACK * c0 : PACK * c1],
+                out=we_words[w][:, c0:c1].bitcast(FP8X4), scales=we_scales[w][:, c0:c1],
+                in_=we_bf[w][:, PACK * c0 : PACK * c1],
             )
 
-        def interleaved(bank, width):
-            return bank[:].rearrange("p (t n) -> p n t", n=width)
+        def interleaved(bank):
+            return bank[:].rearrange("p (t n) -> p n t", n=C)
 
-        def as_nt(ap, width):
-            return ap.rearrange("p (n t) -> p n t", n=width)
+        def as_nt(ap):
+            return ap.rearrange("p (n t) -> p n t", n=C)
 
-        def field(w, c):
-            j0, width, t0 = UNITS[c]
-            cols = slice(j0, j0 + width)
-            bank = banks[F_BANKS[w][c]]
-            for i in range(512 // width):
-                t = t0 + i
+        def edge_bank(w, u):
+            return banks[4 + u % 4 if w == X else u]
+
+        def field(w, u):
+            cols = slice(C * u, C * (u + 1))
+            bank = banks[u if w == Y else u % FX_BANKS]
+            for t in range(PACK):
                 nc.tensor.matmul_mx(
-                    out=bank[:, width * i : width * (i + 1)],
+                    out=bank[:, C * t : C * (t + 1)],
                     lhsT=wf_words[w][:, 2 * P * t : 2 * P * (t + 1)].bitcast(FP4X4),
                     lhsT_scale=wf_scales[w][:, P * t : P * (t + 1)],
                     rhs=gv2_words[:, cols].bitcast(FP8X4),
                     rhs_scale=gv2_scales[:, cols],
                     start=True, stop=True,
                 )
-            nc.scalar.activation(out=as_nt(f_sb[w][c][:], width), in_=interleaved(bank, width), func=ACT.Copy)
+            nc.scalar.activation(out=as_nt(f_sb[w][u][:]), in_=interleaved(bank), func=ACT.Copy)
 
-        def edge(w, c):
-            j0, width, t0 = UNITS[c]
-            cols = slice(j0, j0 + width)
-            bank = banks[E_BANKS[w][c]]
-            passes = ((1, 0), (0, 1))[w]
-            for i in range(512 // width):
-                t = t0 + i
-                for a in passes:
-                    nc.tensor.matmul_mx(
-                        out=bank[:, width * i : width * (i + 1)],
-                        lhsT=we_words[w][a][:, P * t : P * (t + 1)].bitcast(FP8X4),
-                        lhsT_scale=we_scales[w][a][:, P * t : P * (t + 1)],
-                        rhs=gv_words[a][:, cols].bitcast(FP8X4),
-                        rhs_scale=gv_scales[4 * a : P, cols],
-                        start=(a == passes[0]), stop=(a == passes[1]),
-                    )
-            nc.vector.tensor_tensor(
-                out=as_nt(prod[w][:, 512 * c : 512 * (c + 1)], width),
-                in0=interleaved(bank, width), in1=as_nt(f_sb[1 - w][c][:], width), op=ALU.mult,
-            )
-
-        def difference(engine, g, n0, n1):
-            j0, width = GROUPS[g]
-            cols = slice(PACK * j0, PACK * (j0 + width))
-            units = width // P
-            ins = [prod[w][:, cols].rearrange("p (u n t) -> p n u t", u=units, n=width)[:, n0:n1] for w in range(2)]
-            engine.tensor_tensor(
-                out=h_bf[H_BUFS[g]][:, : PACK * width].rearrange("p (n u t) -> p n u t", u=units, n=width)[:, n0:n1],
-                in0=ins[0], in1=ins[1], op=ALU.subtract,
-            )
-
-        def torque(g):
-            j0, width = GROUPS[g]
-            cols = slice(j0, j0 + width)
-            nc.vector.quantize_mx(
-                out=h_words[:, cols].bitcast(FP8X4), scales=h_scales[:, cols],
-                in_=h_bf[H_BUFS[g]][:, : PACK * width],
-            )
-            sums = []
-            for u in range(NT):
-                b, first = divmod(width * u, 512)
-                sums.append(banks[Y_BANKS[g][b]][:, first : first + width])
+        def edge_pass(w, u, a):
+            cols = slice(C * u, C * (u + 1))
+            for t in range(PACK):
                 nc.tensor.matmul_mx(
-                    out=sums[u],
-                    lhsT=wt_w[:, P * u : P * (u + 1)].bitcast(FP8X4),
-                    lhsT_scale=wt_s[:].bitcast(U8)[:, P * u : P * (u + 1)],
-                    rhs=h_words[:, cols].bitcast(FP8X4),
-                    rhs_scale=h_scales[:, cols],
+                    out=edge_bank(w, u)[:, C * t : C * (t + 1)],
+                    lhsT=we_words[w][:, H * a + P * t : H * a + P * (t + 1)].bitcast(FP8X4),
+                    lhsT_scale=we_scales[w][:, H * a + P * t : H * a + P * (t + 1)],
+                    rhs=gv_words[a][:, cols].bitcast(FP8X4),
+                    rhs_scale=gv_scales[4 * a : P, cols],
+                    start=(a == 0 and t == 0), stop=(a == 1 and t == PACK - 1),
+                )
+
+        def product(w, u):
+            nc.vector.tensor_tensor(
+                out=as_nt(prod[w][u]), in0=interleaved(edge_bank(w, u)), in1=as_nt(f_sb[1 - w][u][:]), op=ALU.mult,
+            )
+
+        def difference(u, engine, c0=0, c1=C * PACK):
+            g = [u in units for units in GROUPS].index(True)
+            first = C * PACK * GROUPS[g].index(u)
+            engine.tensor_tensor(
+                out=h_bf[g][:, first + c0 : first + c1], in0=prod[X][u][:, c0:c1], in1=prod[Y][u][:, c0:c1],
+                op=ALU.subtract,
+            )
+
+        def torque(g, on_vector=()):
+            units = GROUPS[g]
+            width = C * len(units)
+            cols = slice(C * units[0], C * units[0] + width)
+            nc.vector.quantize_mx(out=h_words[g][:].bitcast(FP8X4), scales=h_scales[g][:], in_=h_bf[g][:])
+            sums = []
+            for i in range(NT):
+                b, first = divmod(width * i, 512)
+                sums.append(edge_bank(Y, units[b])[:, first : first + width])
+                nc.tensor.matmul_mx(
+                    out=sums[i],
+                    lhsT=wt_w[:, P * i : P * (i + 1)].bitcast(FP8X4),
+                    lhsT_scale=wt_s[:].bitcast(U8)[:, P * i : P * (i + 1)],
+                    rhs=h_words[g][:].bitcast(FP8X4),
+                    rhs_scale=h_scales[g][:],
                     start=True, stop=True,
                 )
-            for u in range(NT):
-                if (g, u) in VECTOR_OUT:
+            for i in range(NT):
+                if i in on_vector:
                     nc.vector.tensor_scalar(
-                        out=y_sb[:, u, cols], in0=sums[u], scalar1=tl_col[:, u : u + 1], scalar2=None, op0=ALU.subtract,
+                        out=y_sb[g][:, i, :], in0=sums[i], scalar1=tl_col[:, i : i + 1], scalar2=None, op0=ALU.subtract,
                     )
                 else:
                     nc.scalar.activation(
-                        out=y_sb[:, u, cols], in_=sums[u], func=ACT.Identity, bias=neg_tl[:, u : u + 1], scale=1.0,
+                        out=y_sb[g][:, i, :], in_=sums[i], func=ACT.Identity, bias=neg_tl[:, i : i + 1], scale=1.0,
                     )
-                if g in STORE_BY_TILE:
-                    nc.sync.dma_start(out=out[P * u : P * (u + 1), cols], in_=y_sb[:, u, cols])
-            if g not in STORE_BY_TILE:
-                nc.sync.dma_start(out=out.rearrange("(u p) n -> p u n", p=P)[:, :, cols], in_=y_sb[:, :, cols])
-
-        def diff_vector(g):
-            difference(nc.vector, g, GP_TOKENS[g], GROUPS[g][1])
-
-        def diff_gpsimd(g):
-            difference(nc.gpsimd, g, 0, GP_TOKENS[g])
+            nc.sync.dma_start(out=out.rearrange("(i p) n -> p i n", p=P)[:, :, cols], in_=y_sb[g][:])
 
         gather(gv2_scales, v2_scales, U8, idx2, 0, S)
-        gather(gv_scales, v_scales, U8, idx, 0, S)
+        permute_words(Y, nc.gpsimd)
+        permute_words(X, nc.gpsimd)
+        cast(X, 0)
         gather(gv2_words, v2_words, U32, idx2, 0, HALF)
-        permute(1)
+        permute_scales(Y, nc.gpsimd)
         gather(gv2_words, v2_words, U32, idx2, HALF, S)
+        permute_scales(X, nc.gpsimd)
+        for w in (Y, X):
+            for u in range(UNITS):
+                field(w, u)
+        cast(X, 1, on_vector=True)
+        quantize_we(X, 0, 2 * H)
         gather(gv_words[0], v_words[0], U32, idx, 0, S)
-        cast(0, 1, 0, P)
-        cast(0, 0, 0, P // 2)
-        cast(0, 0, P // 2, P, False, 2, 4)
-        cast(0, 0, P // 2, P, True, 0, 2)
-        field(1, 0)
-        field(1, 1)
-        field(1, 2)
-        field(1, 3)
-        field(1, 4)
-        field(1, 5)
-        field(1, 6)
-        field(1, 7)
-        permute(0)
-        quantize_we(0, 1)
-        quantize_we(0, 0, 0, H // 2)
-        quantize_we(0, 0, H // 2, H)
-        cast(1, 0, 0, P // 2)
-        cast(1, 0, P // 2, P)
-        cast(1, 1, 0, P // 2)
-        cast(1, 1, P // 2, 3 * P // 4, False, 2, 4)
-        field(0, 0)
-        field(0, 1)
-        field(0, 2)
-        field(0, 3)
-        field(0, 4)
-        field(0, 5)
+        for u in range(4):
+            edge_pass(X, u, 0)
         gather(gv_words[1], v_words[1], U32, idx, 0, HALF)
         gather(gv_words[1], v_words[1], U32, idx, HALF, S)
-        quantize_we(1, 0)
-        cast(1, 1, P // 2, P, True, 0, 2)
-        cast(1, 1, 3 * P // 4, P, True, 2, 4)
-        quantize_we(1, 1, 0, H // 2)
-        quantize_we(1, 1, H // 2, H)
-        edge(0, 0)
-        edge(0, 1)
-        edge(0, 2)
-        edge(0, 3)
-        edge(0, 4)
-        edge(0, 5)
-        edge(0, 6)
-        field(0, 6)
-        edge(0, 7)
-        field(0, 7)
+        cast(Y, 0)
+        cast(Y, 1)
+        quantize_we(Y, 0, H)
+        quantize_we(Y, H, 2 * H)
+        for u in range(UNITS):
+            if u >= 4:
+                edge_pass(X, u, 0)
+            edge_pass(X, u, 1)
+            product(X, u)
+        for u in range(UNITS):
+            edge_pass(Y, u, 0)
         nc.scalar.activation(out=neg_tl[:], in_=tl_col[:], func=ACT.Copy, scale=-1.0)
-        edge(1, 0)
-        edge(1, 1)
-        diff_gpsimd(0)
-        edge(1, 2)
-        edge(1, 3)
-        diff_vector(0)
-        diff_gpsimd(1)
-        edge(1, 4)
-        edge(1, 5)
-        torque(0)
-        diff_vector(1)
-        diff_gpsimd(2)
-        edge(1, 6)
-        edge(1, 7)
+        for u in range(UNITS):
+            edge_pass(Y, u, 1)
+            product(Y, u)
+            if u < 2:
+                difference(u, nc.gpsimd)
+            if u == 5:
+                torque(0)
+                difference(2, nc.gpsimd)
+        difference(3, nc.vector)
+        difference(4, nc.vector)
         torque(1)
-        diff_vector(2)
+        difference(5, nc.vector)
+        difference(6, nc.vector)
         torque(2)
-        diff_vector(3)
-        diff_vector(4)
+        difference(7, nc.vector)
         torque(3)
-        torque(4)
+        torque(4, on_vector=range(NT))

@@ -1,6 +1,7 @@
 from contextlib import ExitStack
 
 import concourse.mybir as mybir
+from concourse.masks import make_identity
 
 K, K2, H, N, T, T2, S = 1024, 512, 512, 384, 4096, 2048, 1024
 FLOPS = 2 * S * (2 * K * H + 2 * K2 * H + H * N)
@@ -26,6 +27,7 @@ X, Y = 0, 1
 GROUPS = ((0, 1), (2, 3), (4, 5), (6,), (7,))
 GPSIMD_UNITS = 3
 FX_BANKS = 4
+TURNED = (2, 3, 4)
 
 
 def tile_list_edge_field_torque_kernel(
@@ -48,14 +50,17 @@ def tile_list_edge_field_torque_kernel(
         v2_words = sb("v2_words", [P, T2], I32)
         v2_scales = sb("v2_scales", [P, T2 // 4], I32)
         gv_words = [sb("gv_words%d" % a, [P, S], U32) for a in range(2)]
-        gv_scales = sb("gv_scales", [P, S], U8)
-        gv_rows = sb("gv_rows", [P, S], U8)
+        ident = sb("ident", [P, P], F32)
         gv2_words = sb("gv2_words", [P, S], U32)
-        gv2_scales = sb("gv2_scales", [P, S], U8)
         wf_words_raw = [sb("wf_words_raw%d" % w, [P, H // 2], I32) for w in range(2)]
         wf_scales_raw = [sb("wf_scales_raw%d" % w, [P, H // 4], I32) for w in range(2)]
         wf_words = [sb("wf_words%d" % w, [P, 2 * H], U8) for w in range(2)]
-        wf_scales = [sb("wf_scales%d" % w, [P, H], U8) for w in range(2)]
+        picked = sb("picked", [P, 2 * S], U8)
+        spread = sb("spread", [P, 2 * H + S], U8)
+        planes = sb("planes", [P, 2 * H + 2 * S], U8)
+        wf_scales = [planes[:, H * w : H * (w + 1)] for w in range(2)]
+        gv2_scales = planes[:, 2 * H : 2 * H + S]
+        gv_scales = planes[:, 2 * H + S :]
         we_raw = [[sb("we_raw%d%d" % (w, a), [P, PACK, H], F32) for a in range(2)] for w in range(2)]
         we_bf = [sb("we_bf%d" % w, [P, 2 * PACK * H], BF16) for w in range(2)]
         we_words = [sb("we_words%d" % w, [P, 2 * H], U32) for w in range(2)]
@@ -70,8 +75,8 @@ def tile_list_edge_field_torque_kernel(
             prod[X][u] = we_raw[Y][0][:, j, :]
         for j, u in enumerate(range(7, UNITS)):
             prod[X][u] = we_raw[Y][1][:, j, :]
-        h_bf = [sb("h_bf%d" % g, [P, len(units) * C * PACK], BF16) for g, units in enumerate(GROUPS)]
-        h_bf[1] = h_bf[0]
+        h_all = sb("h_all", [P, 5 * C * PACK], BF16)
+        h_bf = [h_all[:, C * PACK * first : C * PACK * (first + len(units))] for first, units in zip((1, 3, 0, 3, 0), GROUPS)]
         h_words = [sb("h_words%d" % g, [P, len(units) * C], U32) for g, units in enumerate(GROUPS)]
         h_scales = [sb("h_scales%d" % g, [P, len(units) * C], U8) for g, units in enumerate(GROUPS)]
         y_sb = [sb("y_sb%d" % g, [P, NT, len(units) * C], F32) for g, units in enumerate(GROUPS)]
@@ -94,32 +99,44 @@ def tile_list_edge_field_torque_kernel(
         def load_wf_words(w):
             nc.sync.dma_start(out=wf_words_raw[w][:], in_=(wfx_words, wfy_words)[w][0].bitcast(I32))
 
-        for tile in (v2_scales[:], v_scales[:], wf_scales_raw[Y][:], wf_scales_raw[X][:], gv_scales[:].bitcast(I32), wt_s[:]):
+        for tile in (v2_scales[:], wf_scales_raw[Y][:], wf_scales_raw[X][:], v_scales[:], planes[:].bitcast(I32), wt_s[:]):
             nc.vector.memset(tile, 0)
+        make_identity(nc, ident[:])
 
-        def move_scale_rows(a):
+        def load_spread(tile, dram):
+            rows = dram.rearrange("a q t -> (a q) t").bitcast(I32)
+            nc.sync.dma_start(out=tile[0 : 4 * rows.shape[0] - 3 : 4, :], in_=rows)
+
+        def move_scale_rows(dst, src, a):
             for r in range(4):
                 first = 64 * a + 4 * r
-                nc.sync.dma_start(
-                    out=gv_scales[4 * a + r : P : 32, :].bitcast(I32), in_=gv_rows[first : first + 49 : 16, :].bitcast(I32),
-                )
+                nc.sync.dma_start(out=dst[4 * a + r : P : 32, :].bitcast(I32), in_=src[first : first + 49 : 16, :].bitcast(I32))
 
+        load_words(v2_words, tab2_words, 0, 0, T2 // 2)
+        nc.sync.dma_start(idx2[:], offs2)
+        load_spread(v2_scales, tab2_scales)
+        load_spread(wf_scales_raw[Y], wfy_scales)
+        load_spread(wf_scales_raw[X], wfx_scales)
+        nc.sync.dma_start(idx[:], offs)
+        load_spread(v_scales, tab_scales)
+        load_we(X, 0)
         load_wf_words(Y)
         load_wf_words(X)
-        nc.sync.dma_start(idx2[:], offs2)
-        load_scale_rows(v2_scales, tab2_scales)
-        load_we(X, 0)
-        nc.sync.dma_start(idx[:], offs)
-        nc.sync.dma_start(out=v_scales[0:P:4, :], in_=tab_scales.rearrange("a q t -> (a q) t").bitcast(I32))
-        load_words(v2_words, tab2_words, 0, 0, T2)
-        load_scale_rows(wf_scales_raw[Y], wfy_scales)
+        load_words(v2_words, tab2_words, 0, T2 // 2, T2)
         load_we(X, 1)
-        load_scale_rows(wf_scales_raw[X], wfx_scales)
+        nc.vector.tensor_copy(picked[:, :S], v2_scales[:].bitcast(U8).indirect(idx2[:]))
+        for w in (Y, X):
+            nc.gpsimd.tensor_copy(
+                out=spread[:, H * w : H * (w + 1)].rearrange("p (t m) -> p t m", t=PACK),
+                in_=wf_scales_raw[w][:].bitcast(U8).rearrange("p (m t) -> p t m", t=PACK),
+            )
+        nc.vector.tensor_copy(spread[:, 2 * H :].bitcast(I32), picked[:, :S].bitcast(I32))
+        move_scale_rows(planes[:, : 2 * H + S], spread, 0)
         load_words(v_words[0], tab_words, 0, 0, T // 2)
-        nc.vector.tensor_copy(gv_rows[:], v_scales[:].bitcast(U8).indirect(idx[:]))
-        move_scale_rows(0)
+        nc.vector.tensor_copy(picked[:, S:], v_scales[:].bitcast(U8).indirect(idx[:]))
+        move_scale_rows(gv_scales, picked[:, S:], 0)
         load_words(v_words[0], tab_words, 0, T // 2, T)
-        move_scale_rows(1)
+        move_scale_rows(gv_scales, picked[:, S:], 1)
         load_words(v_words[1], tab_words, 1, 0, T)
         load_we(Y, 0)
         load_we(Y, 1)
@@ -136,12 +153,6 @@ def tile_list_edge_field_torque_kernel(
             engine.tensor_copy(
                 out=wf_words[w][:].bitcast(U16).rearrange("p (t m) -> p t m", t=PACK),
                 in_=wf_words_raw[w][:].bitcast(U16).rearrange("p (m t) -> p t m", t=PACK),
-            )
-
-        def permute_scales(w, engine=nc.vector):
-            engine.tensor_copy(
-                out=wf_scales[w][:].rearrange("p (t m) -> p t m", t=PACK),
-                in_=wf_scales_raw[w][:].bitcast(U8).rearrange("p (m t) -> p t m", t=PACK),
             )
 
         def cast(w, a, on_vector=False, m0=0, m1=P, t0=0, t1=PACK):
@@ -170,6 +181,13 @@ def tile_list_edge_field_torque_kernel(
         def field(w, u):
             cols = slice(C * u, C * (u + 1))
             bank = banks[u if w == Y else u % FX_BANKS]
+            if u in TURNED:
+                nc.tensor.matmul_mx(
+                    out=bank[:], lhsT=gv2_words[:, cols].bitcast(FP8X4), lhsT_scale=gv2_scales[:, cols],
+                    rhs=wf_words[w][:].bitcast(FP4X4), rhs_scale=wf_scales[w][:], start=True, stop=True,
+                )
+                nc.scalar.activation(out=f_sb[w][u][:], in_=bank[:], func=ACT.Copy, scale=(-1.0, 1.0)[w])
+                return
             for t in range(PACK):
                 nc.tensor.matmul_mx(
                     out=bank[:, C * t : C * (t + 1)],
@@ -183,6 +201,13 @@ def tile_list_edge_field_torque_kernel(
 
         def edge_pass(w, u, a):
             cols = slice(C * u, C * (u + 1))
+            if u in TURNED:
+                nc.tensor.matmul_mx(
+                    out=edge_bank(w, u)[:], lhsT=gv_words[a][:, cols].bitcast(FP8X4), lhsT_scale=gv_scales[4 * a : P, cols],
+                    rhs=we_words[w][:, H * a : H * (a + 1)].bitcast(FP8X4), rhs_scale=we_scales[w][:, H * a : H * (a + 1)],
+                    start=(a == 0), stop=(a == 1),
+                )
+                return
             for t in range(PACK):
                 nc.tensor.matmul_mx(
                     out=edge_bank(w, u)[:, C * t : C * (t + 1)],
@@ -194,9 +219,23 @@ def tile_list_edge_field_torque_kernel(
                 )
 
         def product(w, u):
+            if u in TURNED:
+                nc.vector.tensor_tensor(out=prod[w][u], in0=edge_bank(w, u)[:], in1=f_sb[1 - w][u][:], op=ALU.mult)
+                return
             nc.vector.tensor_tensor(
                 out=as_nt(prod[w][u]), in0=interleaved(edge_bank(w, u)), in1=as_nt(f_sb[1 - w][u][:]), op=ALU.mult,
             )
+
+        def turned_sum(u, bank):
+            for t in range(PACK):
+                for w in (X, Y):
+                    nc.tensor.matmul(
+                        bank[:, C * t : C * (t + 1)], lhsT=prod[w][u][:, P * t : P * (t + 1)], rhs=ident[:],
+                        start=(w == X), stop=(w == Y), is_transpose=True,
+                    )
+            g = [u in units for units in GROUPS].index(True)
+            first = C * PACK * GROUPS[g].index(u)
+            nc.scalar.activation(out=as_nt(h_bf[g][:, first : first + C * PACK]), in_=interleaved(bank), func=ACT.Copy)
 
         def difference(u, engine, c0=0, c1=C * PACK):
             g = [u in units for units in GROUPS].index(True)
@@ -206,7 +245,7 @@ def tile_list_edge_field_torque_kernel(
                 op=ALU.subtract,
             )
 
-        def torque(g, on_vector=()):
+        def torque(g, y_banks, on_vector=(), by_tile=False):
             units = GROUPS[g]
             width = C * len(units)
             cols = slice(C * units[0], C * units[0] + width)
@@ -214,7 +253,7 @@ def tile_list_edge_field_torque_kernel(
             sums = []
             for i in range(NT):
                 b, first = divmod(width * i, 512)
-                sums.append(edge_bank(Y, units[b])[:, first : first + width])
+                sums.append(banks[y_banks[b]][:, first : first + width])
                 nc.tensor.matmul_mx(
                     out=sums[i],
                     lhsT=wt_w[:, P * i : P * (i + 1)].bitcast(FP8X4),
@@ -232,16 +271,16 @@ def tile_list_edge_field_torque_kernel(
                     nc.scalar.activation(
                         out=y_sb[g][:, i, :], in_=sums[i], func=ACT.Identity, bias=neg_tl[:, i : i + 1], scale=1.0,
                     )
-            nc.sync.dma_start(out=out.rearrange("(i p) n -> p i n", p=P)[:, :, cols], in_=y_sb[g][:])
+                if by_tile:
+                    nc.sync.dma_start(out=out[P * i : P * (i + 1), cols], in_=y_sb[g][:, i, :])
+            if not by_tile:
+                nc.sync.dma_start(out=out.rearrange("(i p) n -> p i n", p=P)[:, :, cols], in_=y_sb[g][:])
 
-        gather(gv2_scales, v2_scales, U8, idx2, 0, S)
         permute_words(Y, nc.gpsimd)
         permute_words(X, nc.gpsimd)
         cast(X, 0)
         gather(gv2_words, v2_words, U32, idx2, 0, HALF)
-        permute_scales(Y, nc.gpsimd)
         gather(gv2_words, v2_words, U32, idx2, HALF, S)
-        permute_scales(X, nc.gpsimd)
         for w in (Y, X):
             for u in range(UNITS):
                 field(w, u)
@@ -266,18 +305,20 @@ def tile_list_edge_field_torque_kernel(
         nc.scalar.activation(out=neg_tl[:], in_=tl_col[:], func=ACT.Copy, scale=-1.0)
         for u in range(UNITS):
             edge_pass(Y, u, 1)
+        for u in range(UNITS):
             product(Y, u)
             if u < 2:
                 difference(u, nc.gpsimd)
+            if u in (2, 3):
+                turned_sum(u, banks[u - 2])
+            if u == 4:
+                turned_sum(4, banks[2])
             if u == 5:
-                torque(0)
-                difference(2, nc.gpsimd)
-        difference(3, nc.vector)
-        difference(4, nc.vector)
-        torque(1)
-        difference(5, nc.vector)
+                torque(0, (3, 4))
+                difference(5, nc.gpsimd)
+        torque(1, (0, 1))
         difference(6, nc.vector)
-        torque(2)
+        torque(2, (5, 6), by_tile=True)
         difference(7, nc.vector)
-        torque(3)
-        torque(4, on_vector=range(NT))
+        torque(3, (7,))
+        torque(4, (2,), on_vector=range(NT))

@@ -71,12 +71,12 @@ def tile_list_edge_field_torque_kernel(
         neg_tl = sb("neg_tl", [P, NT], F32)
         f_sb = [[sb("f_sb%d%d" % (w, u), [P, C * PACK], F32) for u in range(UNITS)] for w in range(2)]
         prod = [[sb("prod%d%d" % (w, u), [P, C * PACK], F32)[:] for u in range(UNITS)] for w in range(2)]
-        for j, u in enumerate(range(5, 7)):
+        for j, u in enumerate(range(5, 6)):
             prod[X][u] = we_raw[Y][0][:, j, :]
-        for j, u in enumerate(range(7, UNITS)):
+        for j, u in enumerate(range(6, UNITS)):
             prod[X][u] = we_raw[Y][1][:, j, :]
         h_all = sb("h_all", [P, 5 * C * PACK], BF16)
-        h_bf = [h_all[:, C * PACK * first : C * PACK * (first + len(units))] for first, units in zip((1, 3, 0, 3, 0), GROUPS)]
+        h_bf = [h_all[:, C * PACK * first : C * PACK * (first + len(units))] for first, units in zip((1, 3, 0, 0, 1), GROUPS)]
         h_words = [sb("h_words%d" % g, [P, len(units) * C], U32) for g, units in enumerate(GROUPS)]
         h_scales = [sb("h_scales%d" % g, [P, len(units) * C], U8) for g, units in enumerate(GROUPS)]
         y_sb = [sb("y_sb%d" % g, [P, NT, len(units) * C], F32) for g, units in enumerate(GROUPS)]
@@ -278,21 +278,25 @@ def tile_list_edge_field_torque_kernel(
 
         permute_words(Y, nc.gpsimd)
         permute_words(X, nc.gpsimd)
-        cast(X, 0)
+        cast(X, 0, t1=2)
+        cast(X, 0, t0=2)
         gather(gv2_words, v2_words, U32, idx2, 0, HALF)
         gather(gv2_words, v2_words, U32, idx2, HALF, S)
         for w in (Y, X):
             for u in range(UNITS):
                 field(w, u)
-        cast(X, 1, on_vector=True)
+        cast(X, 1, on_vector=True, t1=2)
+        cast(X, 1, on_vector=True, t0=2)
         quantize_we(X, 0, 2 * H)
         gather(gv_words[0], v_words[0], U32, idx, 0, S)
         for u in range(4):
             edge_pass(X, u, 0)
         gather(gv_words[1], v_words[1], U32, idx, 0, HALF)
         gather(gv_words[1], v_words[1], U32, idx, HALF, S)
-        cast(Y, 0)
-        cast(Y, 1)
+        cast(Y, 0, t1=2)
+        cast(Y, 0, t0=2)
+        cast(Y, 1, t0=2)
+        cast(Y, 1, on_vector=True, t1=2)
         quantize_we(Y, 0, H)
         quantize_we(Y, H, 2 * H)
         for u in range(UNITS):
@@ -314,11 +318,11 @@ def tile_list_edge_field_torque_kernel(
             if u == 4:
                 turned_sum(4, banks[2])
             if u == 5:
-                torque(0, (3, 4))
+                torque(0, (3, 4), by_tile=True)
                 difference(5, nc.gpsimd)
-        torque(1, (0, 1))
-        difference(6, nc.vector)
+        torque(1, (0, 1), by_tile=True)
         torque(2, (5, 6), by_tile=True)
+        difference(6, nc.vector)
         difference(7, nc.vector)
-        torque(3, (7,))
-        torque(4, (2,), on_vector=range(NT))
+        torque(3, (7,), on_vector=range(NT))
+        torque(4, (2,))

@@ -126,7 +126,7 @@ def tile_list_edge_field_torque_kernel(
         load_we(X, 1)
         nc.vector.tensor_copy(picked[:, :S], v2_scales[:].bitcast(U8).indirect(idx2[:]))
         for w in (Y, X):
-            nc.gpsimd.tensor_copy(
+            nc.vector.tensor_copy(
                 out=spread[:, H * w : H * (w + 1)].rearrange("p (t m) -> p t m", t=PACK),
                 in_=wf_scales_raw[w][:].bitcast(U8).rearrange("p (m t) -> p t m", t=PACK),
             )
@@ -276,8 +276,8 @@ def tile_list_edge_field_torque_kernel(
             if not by_tile:
                 nc.sync.dma_start(out=out.rearrange("(i p) n -> p i n", p=P)[:, :, cols], in_=y_sb[g][:])
 
-        permute_words(Y, nc.gpsimd)
-        permute_words(X, nc.gpsimd)
+        permute_words(Y)
+        permute_words(X)
         cast(X, 0, t1=2)
         cast(X, 0, t0=2)
         gather(gv2_words, v2_words, U32, idx2, 0, HALF)

@@ -20,14 +20,22 @@ ACT = mybir.ActivationFunctionType
 P = 128
 PACK = 4
 C = 128
+W = C * PACK
 UNITS = S // C
+LAST = UNITS - 1
 HALF = S // 2
 NT = N // P
 X, Y = 0, 1
+
 GROUPS = ((0, 1), (2, 3), (4, 5), (6,), (7,))
-GPSIMD_UNITS = 3
-FX_BANKS = 4
 TURNED = (2, 3, 4)
+V_PLANES = (4, 8)
+
+FX_BANKS = 4
+EY_AHEAD = 5
+EY_BANKS = (0, 1, 2, 3, 6, 0, 1, 2)
+SUM_BANKS = {2: 4, 3: 5, 4: 3}
+OUT_BANKS = ((4, 6), (5, 0), (3, 1), (2,), (7,))
 
 
 def tile_list_edge_field_torque_kernel(
@@ -38,7 +46,7 @@ def tile_list_edge_field_torque_kernel(
     with ExitStack() as ctx:
         keep = ctx.enter_context(tc.tile_pool(name="keep", bufs=1))
         psum = ctx.enter_context(tc.psum_pool(name="psum", bufs=1))
-        banks = [psum.tile([P, 512], F32, name="bank%d" % b) for b in range(8)]
+        banks = [psum.tile([P, W], F32, name="bank%d" % b) for b in range(8)]
 
         def sb(name, shape, dtype):
             return keep.tile(shape, dtype, name=name, align_bytes=64)
@@ -50,17 +58,15 @@ def tile_list_edge_field_torque_kernel(
         v2_words = sb("v2_words", [P, T2], I32)
         v2_scales = sb("v2_scales", [P, T2 // 4], I32)
         gv_words = [sb("gv_words%d" % a, [P, S], U32) for a in range(2)]
-        ident = sb("ident", [P, P], F32)
         gv2_words = sb("gv2_words", [P, S], U32)
+        picked = sb("picked", [P, 2 * S], U8)
+        gv_scales = [sb("gv_scales%d" % a, [P, S], U8) for a in range(2)]
         wf_words_raw = [sb("wf_words_raw%d" % w, [P, H // 2], I32) for w in range(2)]
         wf_scales_raw = [sb("wf_scales_raw%d" % w, [P, H // 4], I32) for w in range(2)]
         wf_words = [sb("wf_words%d" % w, [P, 2 * H], U8) for w in range(2)]
-        picked = sb("picked", [P, 2 * S], U8)
-        spread = sb("spread", [P, 2 * H + S], U8)
-        planes = sb("planes", [P, 2 * H + 2 * S], U8)
-        wf_scales = [planes[:, H * w : H * (w + 1)] for w in range(2)]
-        gv2_scales = planes[:, 2 * H : 2 * H + S]
-        gv_scales = planes[:, 2 * H + S :]
+        field_planes = sb("field_planes", [P, 2 * H + S], U8)
+        wf_scales = [field_planes[:, H * w : H * (w + 1)] for w in range(2)]
+        gv2_scales = field_planes[:, 2 * H :]
         we_raw = [[sb("we_raw%d%d" % (w, a), [P, PACK, H], F32) for a in range(2)] for w in range(2)]
         we_bf = [sb("we_bf%d" % w, [P, 2 * PACK * H], BF16) for w in range(2)]
         we_words = [sb("we_words%d" % w, [P, 2 * H], U32) for w in range(2)]
@@ -69,99 +75,102 @@ def tile_list_edge_field_torque_kernel(
         wt_s = sb("wt_s", [P, N // 4], I32)
         tl_col = sb("tl_col", [P, NT], F32)
         neg_tl = sb("neg_tl", [P, NT], F32)
-        f_sb = [[sb("f_sb%d%d" % (w, u), [P, C * PACK], F32) for u in range(UNITS)] for w in range(2)]
-        prod = [[sb("prod%d%d" % (w, u), [P, C * PACK], F32)[:] for u in range(UNITS)] for w in range(2)]
-        for j, u in enumerate(range(5, 6)):
-            prod[X][u] = we_raw[Y][0][:, j, :]
-        for j, u in enumerate(range(6, UNITS)):
-            prod[X][u] = we_raw[Y][1][:, j, :]
-        h_all = sb("h_all", [P, 5 * C * PACK], BF16)
-        h_bf = [h_all[:, C * PACK * first : C * PACK * (first + len(units))] for first, units in zip((1, 3, 0, 0, 1), GROUPS)]
+        ident = sb("ident", [P, P], F32)
+        f_sb = [[sb("f_sb%d%d" % (w, u), [P, W], F32) for u in range(UNITS)] for w in range(2)]
+
+        h_all = sb("h_all", [P, 6 * W], BF16)
+        h_bf = [h_all[:, W * slot : W * (slot + len(units))] for slot, units in zip((1, 4, 0, 0, 1), GROUPS)]
+        prod = [
+            [sb("prod_x%d" % u, [P, W], F32)[:] for u in range(UNITS - 2)]
+            + [we_raw[Y][1][:, 0, :], h_all[:, 2 * W : 4 * W].bitcast(F32)],
+            [sb("prod_y%d" % u, [P, W], F32)[:] for u in range(UNITS)],
+        ]
         h_words = [sb("h_words%d" % g, [P, len(units) * C], U32) for g, units in enumerate(GROUPS)]
         h_scales = [sb("h_scales%d" % g, [P, len(units) * C], U8) for g, units in enumerate(GROUPS)]
         y_sb = [sb("y_sb%d" % g, [P, NT, len(units) * C], F32) for g, units in enumerate(GROUPS)]
 
-        def words_of(dram, a):
-            return dram[a].rearrange("p t i -> p (t i)").bitcast(I32)
+        def load_words(tile, dram, a, c0, c1):
+            words = dram[a].rearrange("p t i -> p (t i)").bitcast(I32)
+            nc.sync.dma_start(out=tile[:, c0:c1], in_=words[:, c0:c1])
 
-        def load_scale_rows(tile, dram, queue=nc.sync, rows=range(4)):
-            for r in rows:
-                for a in range(dram.shape[0]):
-                    queue.dma_start(out=tile[4 * a + r : P : 32, :], in_=dram[a, r:16:4, :].bitcast(I32))
-
-        def load_words(tile, dram, a, t0, t1):
-            nc.sync.dma_start(out=tile[:, t0:t1], in_=words_of(dram, a)[:, t0:t1])
-
-        def load_we(w, a, c0=0, c1=H):
-            rows = (wex, wey)[w][512 * a : 512 * (a + 1), c0:c1]
-            nc.sync.dma_start(out=we_raw[w][a][:, :, c0:c1], in_=rows.rearrange("(p j) c -> p j c", j=PACK))
+        def load_we(w, a):
+            rows = (wex, wey)[w][512 * a : 512 * (a + 1), :]
+            nc.sync.dma_start(out=we_raw[w][a][:], in_=rows.rearrange("(p j) c -> p j c", j=PACK))
 
         def load_wf_words(w):
             nc.sync.dma_start(out=wf_words_raw[w][:], in_=(wfx_words, wfy_words)[w][0].bitcast(I32))
 
-        for tile in (v2_scales[:], wf_scales_raw[Y][:], wf_scales_raw[X][:], v_scales[:], planes[:].bitcast(I32), wt_s[:]):
-            nc.vector.memset(tile, 0)
-        make_identity(nc, ident[:])
-
-        def load_spread(tile, dram):
+        def load_scale_rows_apart(tile, dram):
             rows = dram.rearrange("a q t -> (a q) t").bitcast(I32)
-            nc.sync.dma_start(out=tile[0 : 4 * rows.shape[0] - 3 : 4, :], in_=rows)
+            nc.sync.dma_start(out=tile[0 : P : P // rows.shape[0], :], in_=rows)
 
-        def move_scale_rows(dst, src, a):
+        def move_field_scale_rows():
+            for r in range(1, 4):
+                nc.sync.dma_start(
+                    out=field_planes[r:P:32, :].bitcast(I32), in_=field_planes[8 * r : P : 32, :].bitcast(I32),
+                )
+
+        def move_edge_scale_rows(a):
             for r in range(4):
                 first = 64 * a + 4 * r
-                nc.sync.dma_start(out=dst[4 * a + r : P : 32, :].bitcast(I32), in_=src[first : first + 49 : 16, :].bitcast(I32))
+                nc.sync.dma_start(
+                    out=gv_scales[a][V_PLANES[a] + r : P : 32, :].bitcast(I32),
+                    in_=picked[first : first + 3 * 16 + 1 : 16, S:].bitcast(I32),
+                )
+
+        def gather(dst, window, dtype, offsets, j0, j1):
+            nc.vector.tensor_copy(dst[:, j0:j1], window[:].bitcast(dtype).indirect(offsets[:, j0 // 16 : j1 // 16]))
+
+        def to_tm_order(dst, src):
+            nc.vector.tensor_copy(
+                out=dst.rearrange("p (t m) -> p t m", t=PACK), in_=src.rearrange("p (m t) -> p t m", t=PACK),
+            )
+
+        for tile in (v2_scales, wf_scales_raw[Y], wf_scales_raw[X], v_scales):
+            nc.vector.memset(tile[:], 0)
+        for a in range(2):
+            nc.vector.memset(gv_scales[a][:].bitcast(I32), 0)
+        nc.vector.memset(wt_s[:], 0)
+        make_identity(nc, ident[:])
 
         load_words(v2_words, tab2_words, 0, 0, T2 // 2)
         nc.sync.dma_start(idx2[:], offs2)
-        load_spread(v2_scales, tab2_scales)
-        load_spread(wf_scales_raw[Y], wfy_scales)
-        load_spread(wf_scales_raw[X], wfx_scales)
+        load_scale_rows_apart(v2_scales, tab2_scales)
+        load_scale_rows_apart(wf_scales_raw[Y], wfy_scales)
+        load_scale_rows_apart(wf_scales_raw[X], wfx_scales)
         nc.sync.dma_start(idx[:], offs)
-        load_spread(v_scales, tab_scales)
         load_we(X, 0)
+        load_scale_rows_apart(v_scales, tab_scales)
         load_wf_words(Y)
         load_wf_words(X)
         load_words(v2_words, tab2_words, 0, T2 // 2, T2)
         load_we(X, 1)
-        nc.vector.tensor_copy(picked[:, :S], v2_scales[:].bitcast(U8).indirect(idx2[:]))
+        gather(picked, v2_scales, U8, idx2, 0, S)
         for w in (Y, X):
-            nc.vector.tensor_copy(
-                out=spread[:, H * w : H * (w + 1)].rearrange("p (t m) -> p t m", t=PACK),
-                in_=wf_scales_raw[w][:].bitcast(U8).rearrange("p (m t) -> p t m", t=PACK),
-            )
-        nc.vector.tensor_copy(spread[:, 2 * H :].bitcast(I32), picked[:, :S].bitcast(I32))
-        move_scale_rows(planes[:, : 2 * H + S], spread, 0)
+            to_tm_order(wf_scales[w], wf_scales_raw[w][:].bitcast(U8))
+        nc.vector.tensor_copy(gv2_scales.bitcast(I32), picked[:, :S].bitcast(I32))
+        move_field_scale_rows()
         load_words(v_words[0], tab_words, 0, 0, T // 2)
-        nc.vector.tensor_copy(picked[:, S:], v_scales[:].bitcast(U8).indirect(idx[:]))
-        move_scale_rows(gv_scales, picked[:, S:], 0)
+        gather(picked[:, S:], v_scales, U8, idx, 0, S)
+        move_edge_scale_rows(0)
         load_words(v_words[0], tab_words, 0, T // 2, T)
-        move_scale_rows(gv_scales, picked[:, S:], 1)
         load_words(v_words[1], tab_words, 1, 0, T)
+        move_edge_scale_rows(1)
         load_we(Y, 0)
         load_we(Y, 1)
         load_words(wt_w, wt_words, 0, 0, N)
-        load_scale_rows(wt_s, wt_scales)
+        for r in range(4):
+            nc.sync.dma_start(out=wt_s[r:P:32, :], in_=wt_scales[0, r:16:4, :].bitcast(I32))
         with nc.allow_non_contiguous_dma(reason="one value of tl to a partition"):
             nc.sync.dma_start(out=tl_col[:], in_=tl.rearrange("(c p) -> p c", p=P))
 
-        def gather(dst, window, dtype, offsets, j0, j1):
-            entries = offsets[:, j0 // 16 : j1 // 16]
-            nc.vector.tensor_copy(dst[:, j0:j1], window[:].bitcast(dtype).indirect(entries))
-
-        def permute_words(w, engine=nc.vector):
-            engine.tensor_copy(
-                out=wf_words[w][:].bitcast(U16).rearrange("p (t m) -> p t m", t=PACK),
-                in_=wf_words_raw[w][:].bitcast(U16).rearrange("p (m t) -> p t m", t=PACK),
-            )
-
-        def cast(w, a, on_vector=False, m0=0, m1=P, t0=0, t1=PACK):
-            dst = we_bf[w][:, PACK * H * a : PACK * H * (a + 1)].rearrange("p (t m j) -> p m j t", t=PACK, j=PACK)[:, m0:m1, :, t0:t1]
-            src = we_raw[w][a][:].rearrange("p j (m t) -> p m j t", t=PACK)[:, m0:m1, :, t0:t1]
+        def cast(w, a, t0, on_vector=False):
+            dst = we_bf[w][:, PACK * H * a : PACK * H * (a + 1)].rearrange("p (t m j) -> p m j t", t=PACK, j=PACK)
+            src = we_raw[w][a][:].rearrange("p j (m t) -> p m j t", t=PACK)
             if on_vector:
-                nc.vector.tensor_copy(out=dst, in_=src)
+                nc.vector.tensor_copy(out=dst[:, :, :, t0 : t0 + 2], in_=src[:, :, :, t0 : t0 + 2])
             else:
-                nc.scalar.activation(out=dst, in_=src, func=ACT.Copy)
+                nc.scalar.activation(out=dst[:, :, :, t0 : t0 + 2], in_=src[:, :, :, t0 : t0 + 2], func=ACT.Copy)
 
         def quantize_we(w, c0, c1):
             nc.vector.quantize_mx(
@@ -169,14 +178,14 @@ def tile_list_edge_field_torque_kernel(
                 in_=we_bf[w][:, PACK * c0 : PACK * c1],
             )
 
-        def interleaved(bank):
+        def bank_as_nt(bank):
             return bank[:].rearrange("p (t n) -> p n t", n=C)
 
         def as_nt(ap):
             return ap.rearrange("p (n t) -> p n t", n=C)
 
         def edge_bank(w, u):
-            return banks[4 + u % 4 if w == X else u]
+            return banks[FX_BANKS + u % FX_BANKS if w == X else EY_BANKS[u]]
 
         def field(w, u):
             cols = slice(C * u, C * (u + 1))
@@ -184,9 +193,9 @@ def tile_list_edge_field_torque_kernel(
             if u in TURNED:
                 nc.tensor.matmul_mx(
                     out=bank[:], lhsT=gv2_words[:, cols].bitcast(FP8X4), lhsT_scale=gv2_scales[:, cols],
-                    rhs=wf_words[w][:].bitcast(FP4X4), rhs_scale=wf_scales[w][:], start=True, stop=True,
+                    rhs=wf_words[w][:].bitcast(FP4X4), rhs_scale=wf_scales[w], start=True, stop=True,
                 )
-                nc.scalar.activation(out=f_sb[w][u][:], in_=bank[:], func=ACT.Copy, scale=(-1.0, 1.0)[w])
+                nc.scalar.activation(out=f_sb[w][u][:], in_=bank[:], func=ACT.Copy, scale=-1.0 if w == X else 1.0)
                 return
             for t in range(PACK):
                 nc.tensor.matmul_mx(
@@ -197,24 +206,25 @@ def tile_list_edge_field_torque_kernel(
                     rhs_scale=gv2_scales[:, cols],
                     start=True, stop=True,
                 )
-            nc.scalar.activation(out=as_nt(f_sb[w][u][:]), in_=interleaved(bank), func=ACT.Copy)
+            nc.scalar.activation(out=as_nt(f_sb[w][u][:]), in_=bank_as_nt(bank), func=ACT.Copy)
 
         def edge_pass(w, u, a):
             cols = slice(C * u, C * (u + 1))
+            entries = gv_words[a][:, cols].bitcast(FP8X4)
+            entry_scales = gv_scales[a][V_PLANES[a] : P, cols]
             if u in TURNED:
                 nc.tensor.matmul_mx(
-                    out=edge_bank(w, u)[:], lhsT=gv_words[a][:, cols].bitcast(FP8X4), lhsT_scale=gv_scales[4 * a : P, cols],
+                    out=edge_bank(w, u)[:], lhsT=entries, lhsT_scale=entry_scales,
                     rhs=we_words[w][:, H * a : H * (a + 1)].bitcast(FP8X4), rhs_scale=we_scales[w][:, H * a : H * (a + 1)],
                     start=(a == 0), stop=(a == 1),
                 )
                 return
             for t in range(PACK):
+                wcols = slice(H * a + P * t, H * a + P * (t + 1))
                 nc.tensor.matmul_mx(
                     out=edge_bank(w, u)[:, C * t : C * (t + 1)],
-                    lhsT=we_words[w][:, H * a + P * t : H * a + P * (t + 1)].bitcast(FP8X4),
-                    lhsT_scale=we_scales[w][:, H * a + P * t : H * a + P * (t + 1)],
-                    rhs=gv_words[a][:, cols].bitcast(FP8X4),
-                    rhs_scale=gv_scales[4 * a : P, cols],
+                    lhsT=we_words[w][:, wcols].bitcast(FP8X4), lhsT_scale=we_scales[w][:, wcols],
+                    rhs=entries, rhs_scale=entry_scales,
                     start=(a == 0 and t == 0), stop=(a == 1 and t == PACK - 1),
                 )
 
@@ -223,37 +233,36 @@ def tile_list_edge_field_torque_kernel(
                 nc.vector.tensor_tensor(out=prod[w][u], in0=edge_bank(w, u)[:], in1=f_sb[1 - w][u][:], op=ALU.mult)
                 return
             nc.vector.tensor_tensor(
-                out=as_nt(prod[w][u]), in0=interleaved(edge_bank(w, u)), in1=as_nt(f_sb[1 - w][u][:]), op=ALU.mult,
+                out=as_nt(prod[w][u]), in0=bank_as_nt(edge_bank(w, u)), in1=as_nt(f_sb[1 - w][u][:]), op=ALU.mult,
             )
 
-        def turned_sum(u, bank):
+        def h_of(u):
+            g = [u in units for units in GROUPS].index(True)
+            first = W * GROUPS[g].index(u)
+            return h_bf[g][:, first : first + W]
+
+        def turn(w, u):
             for t in range(PACK):
-                for w in (X, Y):
-                    nc.tensor.matmul(
-                        bank[:, C * t : C * (t + 1)], lhsT=prod[w][u][:, P * t : P * (t + 1)], rhs=ident[:],
-                        start=(w == X), stop=(w == Y), is_transpose=True,
-                    )
-            g = [u in units for units in GROUPS].index(True)
-            first = C * PACK * GROUPS[g].index(u)
-            nc.scalar.activation(out=as_nt(h_bf[g][:, first : first + C * PACK]), in_=interleaved(bank), func=ACT.Copy)
+                nc.tensor.matmul(
+                    banks[SUM_BANKS[u]][:, C * t : C * (t + 1)], lhsT=prod[w][u][:, P * t : P * (t + 1)], rhs=ident[:],
+                    start=(w == X and t == 0), stop=(w == Y and t == PACK - 1), is_transpose=True,
+                )
 
-        def difference(u, engine, c0=0, c1=C * PACK):
-            g = [u in units for units in GROUPS].index(True)
-            first = C * PACK * GROUPS[g].index(u)
-            engine.tensor_tensor(
-                out=h_bf[g][:, first + c0 : first + c1], in0=prod[X][u][:, c0:c1], in1=prod[Y][u][:, c0:c1],
-                op=ALU.subtract,
-            )
+        def turned_out(u):
+            nc.scalar.activation(out=as_nt(h_of(u)), in_=bank_as_nt(banks[SUM_BANKS[u]]), func=ACT.Copy)
 
-        def torque(g, y_banks, on_vector=(), by_tile=False):
+        def difference(u, engine):
+            engine.tensor_tensor(out=h_of(u), in0=prod[X][u], in1=prod[Y][u], op=ALU.subtract)
+
+        def torque(g, on_vector=False):
             units = GROUPS[g]
             width = C * len(units)
             cols = slice(C * units[0], C * units[0] + width)
-            nc.vector.quantize_mx(out=h_words[g][:].bitcast(FP8X4), scales=h_scales[g][:], in_=h_bf[g][:])
+            nc.vector.quantize_mx(out=h_words[g][:].bitcast(FP8X4), scales=h_scales[g][:], in_=h_bf[g])
             sums = []
             for i in range(NT):
-                b, first = divmod(width * i, 512)
-                sums.append(banks[y_banks[b]][:, first : first + width])
+                b, first = divmod(width * i, W)
+                sums.append(banks[OUT_BANKS[g][b]][:, first : first + width])
                 nc.tensor.matmul_mx(
                     out=sums[i],
                     lhsT=wt_w[:, P * i : P * (i + 1)].bitcast(FP8X4),
@@ -263,7 +272,7 @@ def tile_list_edge_field_torque_kernel(
                     start=True, stop=True,
                 )
             for i in range(NT):
-                if i in on_vector:
+                if on_vector:
                     nc.vector.tensor_scalar(
                         out=y_sb[g][:, i, :], in0=sums[i], scalar1=tl_col[:, i : i + 1], scalar2=None, op0=ALU.subtract,
                     )
@@ -271,58 +280,69 @@ def tile_list_edge_field_torque_kernel(
                     nc.scalar.activation(
                         out=y_sb[g][:, i, :], in_=sums[i], func=ACT.Identity, bias=neg_tl[:, i : i + 1], scale=1.0,
                     )
-                if by_tile:
+                if len(units) > 1:
                     nc.sync.dma_start(out=out[P * i : P * (i + 1), cols], in_=y_sb[g][:, i, :])
-            if not by_tile:
+            if len(units) == 1:
                 nc.sync.dma_start(out=out.rearrange("(i p) n -> p i n", p=P)[:, :, cols], in_=y_sb[g][:])
 
-        permute_words(Y)
-        permute_words(X)
-        cast(X, 0, t1=2)
-        cast(X, 0, t0=2)
+        for w in (Y, X):
+            to_tm_order(wf_words[w][:].bitcast(U16), wf_words_raw[w][:].bitcast(U16))
+        cast(X, 0, 0)
+        cast(X, 0, 2)
         gather(gv2_words, v2_words, U32, idx2, 0, HALF)
         gather(gv2_words, v2_words, U32, idx2, HALF, S)
         for w in (Y, X):
             for u in range(UNITS):
                 field(w, u)
-        cast(X, 1, on_vector=True, t1=2)
-        cast(X, 1, on_vector=True, t0=2)
+        cast(X, 1, 0, on_vector=True)
+        cast(X, 1, 2, on_vector=True)
         quantize_we(X, 0, 2 * H)
+
         gather(gv_words[0], v_words[0], U32, idx, 0, S)
-        for u in range(4):
+        for u in range(FX_BANKS):
             edge_pass(X, u, 0)
         gather(gv_words[1], v_words[1], U32, idx, 0, HALF)
         gather(gv_words[1], v_words[1], U32, idx, HALF, S)
-        cast(Y, 0, t1=2)
-        cast(Y, 0, t0=2)
-        cast(Y, 1, t0=2)
-        cast(Y, 1, on_vector=True, t1=2)
+
+        cast(Y, 0, 0)
+        cast(Y, 0, 2)
+        cast(Y, 1, 2)
+        cast(Y, 1, 0, on_vector=True)
         quantize_we(Y, 0, H)
         quantize_we(Y, H, 2 * H)
+
         for u in range(UNITS):
-            if u >= 4:
+            if u >= FX_BANKS:
                 edge_pass(X, u, 0)
             edge_pass(X, u, 1)
-            product(X, u)
-        for u in range(UNITS):
-            edge_pass(Y, u, 0)
+            if u < LAST:
+                product(X, u)
+        for u in TURNED[:2]:
+            turn(X, u)
         nc.scalar.activation(out=neg_tl[:], in_=tl_col[:], func=ACT.Copy, scale=-1.0)
-        for u in range(UNITS):
-            edge_pass(Y, u, 1)
+
+        for a in range(2):
+            for u in range(EY_AHEAD):
+                edge_pass(Y, u, a)
         for u in range(UNITS):
             product(Y, u)
-            if u < 2:
+            if EY_AHEAD + u < UNITS:
+                edge_pass(Y, EY_AHEAD + u, 0)
+                edge_pass(Y, EY_AHEAD + u, 1)
+            if u in GROUPS[0]:
                 difference(u, nc.gpsimd)
-            if u in (2, 3):
-                turned_sum(u, banks[u - 2])
-            if u == 4:
-                turned_sum(4, banks[2])
-            if u == 5:
-                torque(0, (3, 4), by_tile=True)
-                difference(5, nc.gpsimd)
-        torque(1, (0, 1), by_tile=True)
-        torque(2, (5, 6), by_tile=True)
-        difference(6, nc.vector)
-        difference(7, nc.vector)
-        torque(3, (7,), on_vector=range(NT))
-        torque(4, (2,))
+            if u == TURNED[-1]:
+                turn(X, u)
+            if u in TURNED:
+                turn(Y, u)
+                turned_out(u)
+            if u == GROUPS[2][1]:
+                torque(0)
+                difference(u, nc.gpsimd)
+        product(X, LAST)
+        torque(1)
+        torque(2)
+        difference(LAST - 1, nc.vector)
+        difference(LAST, nc.vector)
+        torque(3, on_vector=True)
+        torque(4)

@@ -33,9 +33,9 @@ V_PLANES = (4, 8)
 
 FX_BANKS = 4
 EY_AHEAD = 5
-EY_BANKS = (0, 1, 2, 3, 6, 0, 1, 2)
-SUM_BANKS = {2: 4, 3: 5, 4: 3}
-OUT_BANKS = ((4, 6), (5, 0), (3, 1), (2,), (7,))
+EY_BANKS = (0, 1, 2, 3, 6, 0, 1, 3)
+SUM_BANKS = {2: 4, 3: 5, 4: 2}
+OUT_BANKS = ((4, 6), (5, 0), (2, 1), (3,), (7,))
 
 
 def tile_list_edge_field_torque_kernel(
@@ -326,9 +326,6 @@ def tile_list_edge_field_torque_kernel(
                 edge_pass(Y, u, a)
         for u in range(UNITS):
             product(Y, u)
-            if EY_AHEAD + u < UNITS:
-                edge_pass(Y, EY_AHEAD + u, 0)
-                edge_pass(Y, EY_AHEAD + u, 1)
             if u in GROUPS[0]:
                 difference(u, nc.gpsimd)
             if u == TURNED[-1]:
@@ -336,10 +333,18 @@ def tile_list_edge_field_torque_kernel(
             if u in TURNED:
                 turn(Y, u)
                 turned_out(u)
+            if u < FX_BANKS and u in EY_BANKS[EY_AHEAD:]:
+                later = EY_AHEAD + EY_BANKS[EY_AHEAD:].index(u)
+                edge_pass(Y, later, 0)
+                edge_pass(Y, later, 1)
             if u == GROUPS[2][1]:
                 torque(0)
                 difference(u, nc.gpsimd)
         product(X, LAST)
+        nc.tensor.matmul_mx(
+            out=edge_bank(X, LAST)[:], lhsT=wt_w[:, :P].bitcast(FP8X4), lhsT_scale=wt_s[:].bitcast(U8)[:, :P],
+            rhs=we_words[Y][:, :H].bitcast(FP8X4), rhs_scale=we_scales[Y][:, :H], start=True, stop=True,
+        )
         torque(1)
         torque(2)
         difference(LAST - 1, nc.vector)

@@ -308,8 +308,8 @@ def tile_list_edge_field_torque_kernel(
         cast(Y, 0, 2)
         cast(Y, 1, 2)
         cast(Y, 1, 0, on_vector=True)
-        quantize_we(Y, 0, H)
-        quantize_we(Y, H, 2 * H)
+        for c0 in range(0, 2 * H, H // 2):
+            quantize_we(Y, c0, c0 + H // 2)
 
         for u in range(UNITS):
             if u >= FX_BANKS:
@@ -341,10 +341,6 @@ def tile_list_edge_field_torque_kernel(
                 torque(0)
                 difference(u, nc.gpsimd)
         product(X, LAST)
-        nc.tensor.matmul_mx(
-            out=edge_bank(X, LAST)[:], lhsT=wt_w[:, :P].bitcast(FP8X4), lhsT_scale=wt_s[:].bitcast(U8)[:, :P],
-            rhs=we_words[Y][:, :H].bitcast(FP8X4), rhs_scale=we_scales[Y][:, :H], start=True, stop=True,
-        )
         torque(1)
         torque(2)
         difference(LAST - 1, nc.vector)

@@ -31,11 +31,13 @@ GROUPS = ((0, 1), (2, 3), (4, 5), (6,), (7,))
 TURNED = (2, 3, 4)
 V_PLANES = (4, 8)
 
+M_SPLIT = 48
+
 FX_BANKS = 4
 EY_AHEAD = 5
-EY_BANKS = (0, 1, 2, 3, 6, 0, 1, 3)
-SUM_BANKS = {2: 4, 3: 5, 4: 2}
-OUT_BANKS = ((4, 6), (5, 0), (2, 1), (3,), (7,))
+EY_BANKS = (6, 7, 0, 1, 2, 3, 6, 7)
+SUM_BANKS = {2: 4, 3: 5, 4: 0}
+OUT_BANKS = ((4, 1), (5, 2), (0, 3), (6,), (7,))
 
 
 def tile_list_edge_field_torque_kernel(
@@ -81,8 +83,9 @@ def tile_list_edge_field_torque_kernel(
         h_all = sb("h_all", [P, 6 * W], BF16)
         h_bf = [h_all[:, W * slot : W * (slot + len(units))] for slot, units in zip((1, 4, 0, 0, 1), GROUPS)]
         prod = [
-            [sb("prod_x%d" % u, [P, W], F32)[:] for u in range(UNITS - 2)]
-            + [we_raw[Y][1][:, 0, :], h_all[:, 2 * W : 4 * W].bitcast(F32)],
+            [sb("prod_x%d" % u, [P, W], F32)[:] for u in range(UNITS // 2)]
+            + [we_raw[Y][0][:, j, :] for j in range(3)]
+            + [we_raw[Y][1][:, 0, :]],
             [sb("prod_y%d" % u, [P, W], F32)[:] for u in range(UNITS)],
         ]
         h_words = [sb("h_words%d" % g, [P, len(units) * C], U32) for g, units in enumerate(GROUPS)]
@@ -140,21 +143,25 @@ def tile_list_edge_field_torque_kernel(
         load_scale_rows_apart(wf_scales_raw[X], wfx_scales)
         nc.sync.dma_start(idx[:], offs)
         load_we(X, 0)
-        load_scale_rows_apart(v_scales, tab_scales)
         load_wf_words(Y)
         load_wf_words(X)
         load_words(v2_words, tab2_words, 0, T2 // 2, T2)
-        load_we(X, 1)
+        load_scale_rows_apart(v_scales, tab_scales)
+        load_words(v_words[0], tab_words, 0, 0, T // 4)
         gather(picked, v2_scales, U8, idx2, 0, S)
         for w in (Y, X):
             to_tm_order(wf_scales[w], wf_scales_raw[w][:].bitcast(U8))
         nc.vector.tensor_copy(gv2_scales.bitcast(I32), picked[:, :S].bitcast(I32))
         move_field_scale_rows()
-        load_words(v_words[0], tab_words, 0, 0, T // 2)
+        load_words(v_words[0], tab_words, 0, T // 4, T)
+        load_words(v_words[1], tab_words, 1, 0, T)
+        for w in (Y, X):
+            to_tm_order(wf_words[w][:].bitcast(U16), wf_words_raw[w][:].bitcast(U16))
+        gather(gv2_words, v2_words, U32, idx2, 0, HALF)
+        gather(gv2_words, v2_words, U32, idx2, HALF, S)
         gather(picked[:, S:], v_scales, U8, idx, 0, S)
         move_edge_scale_rows(0)
-        load_words(v_words[0], tab_words, 0, T // 2, T)
-        load_words(v_words[1], tab_words, 1, 0, T)
+        load_we(X, 1)
         move_edge_scale_rows(1)
         load_we(Y, 0)
         load_we(Y, 1)
@@ -164,13 +171,22 @@ def tile_list_edge_field_torque_kernel(
         with nc.allow_non_contiguous_dma(reason="one value of tl to a partition"):
             nc.sync.dma_start(out=tl_col[:], in_=tl.rearrange("(c p) -> p c", p=P))
 
-        def cast(w, a, t0, on_vector=False):
+        def cast_on_gpsimd(w, a, t0):
+            dst = we_bf[w][:, PACK * H * a : PACK * H * (a + 1)].rearrange("p (t m j) -> p t m j", t=PACK, j=PACK)
+            src = we_raw[w][a][:].rearrange("p j (m t) -> p t m j", t=PACK)
+            nc.gpsimd.tensor_scalar(
+                out=dst[:, t0 : t0 + 2], in0=src[:, t0 : t0 + 2], scalar1=1.0, scalar2=0.0, op0=ALU.mult, op1=ALU.add,
+            )
+
+        def cast(w, a, t0, on_vector=False, m0=0, m1=P):
             dst = we_bf[w][:, PACK * H * a : PACK * H * (a + 1)].rearrange("p (t m j) -> p m j t", t=PACK, j=PACK)
             src = we_raw[w][a][:].rearrange("p j (m t) -> p m j t", t=PACK)
             if on_vector:
-                nc.vector.tensor_copy(out=dst[:, :, :, t0 : t0 + 2], in_=src[:, :, :, t0 : t0 + 2])
+                nc.vector.tensor_copy(out=dst[:, m0:m1, :, t0 : t0 + 2], in_=src[:, m0:m1, :, t0 : t0 + 2])
             else:
-                nc.scalar.activation(out=dst[:, :, :, t0 : t0 + 2], in_=src[:, :, :, t0 : t0 + 2], func=ACT.Copy)
+                nc.scalar.activation(
+                    out=dst[:, m0:m1, :, t0 : t0 + 2], in_=src[:, m0:m1, :, t0 : t0 + 2], func=ACT.Copy,
+                )
 
         def quantize_we(w, c0, c1):
             nc.vector.quantize_mx(
@@ -185,7 +201,7 @@ def tile_list_edge_field_torque_kernel(
             return ap.rearrange("p (n t) -> p n t", n=C)
 
         def edge_bank(w, u):
-            return banks[FX_BANKS + u % FX_BANKS if w == X else EY_BANKS[u]]
+            return banks[(FX_BANKS + u) % UNITS if w == X else EY_BANKS[u]]
 
         def field(w, u):
             cols = slice(C * u, C * (u + 1))
@@ -285,38 +301,33 @@ def tile_list_edge_field_torque_kernel(
             if len(units) == 1:
                 nc.sync.dma_start(out=out.rearrange("(i p) n -> p i n", p=P)[:, :, cols], in_=y_sb[g][:])
 
-        for w in (Y, X):
-            to_tm_order(wf_words[w][:].bitcast(U16), wf_words_raw[w][:].bitcast(U16))
         cast(X, 0, 0)
         cast(X, 0, 2)
-        gather(gv2_words, v2_words, U32, idx2, 0, HALF)
-        gather(gv2_words, v2_words, U32, idx2, HALF, S)
         for w in (Y, X):
             for u in range(UNITS):
                 field(w, u)
-        cast(X, 1, 0, on_vector=True)
-        cast(X, 1, 2, on_vector=True)
-        quantize_we(X, 0, 2 * H)
+        quantize_we(X, 0, H)
 
         gather(gv_words[0], v_words[0], U32, idx, 0, S)
-        for u in range(FX_BANKS):
+        for u in range(UNITS):
             edge_pass(X, u, 0)
-        gather(gv_words[1], v_words[1], U32, idx, 0, HALF)
-        gather(gv_words[1], v_words[1], U32, idx, HALF, S)
+        gather(gv_words[1], v_words[1], U32, idx, 0, S)
+        cast(X, 1, 0, on_vector=True)
+        cast(X, 1, 2, on_vector=True, m1=M_SPLIT)
+        cast(X, 1, 2, m0=M_SPLIT)
+        quantize_we(X, H, H + H // 2)
+        quantize_we(X, H + H // 2, 2 * H)
 
-        cast(Y, 0, 0)
+        cast_on_gpsimd(Y, 0, 0)
         cast(Y, 0, 2)
+        cast(Y, 1, 0)
         cast(Y, 1, 2)
-        cast(Y, 1, 0, on_vector=True)
         for c0 in range(0, 2 * H, H // 2):
             quantize_we(Y, c0, c0 + H // 2)
 
         for u in range(UNITS):
-            if u >= FX_BANKS:
-                edge_pass(X, u, 0)
             edge_pass(X, u, 1)
-            if u < LAST:
-                product(X, u)
+            product(X, u)
         for u in TURNED[:2]:
             turn(X, u)
         nc.scalar.activation(out=neg_tl[:], in_=tl_col[:], func=ACT.Copy, scale=-1.0)
@@ -324,6 +335,8 @@ def tile_list_edge_field_torque_kernel(
         for a in range(2):
             for u in range(EY_AHEAD):
                 edge_pass(Y, u, a)
+        edge_pass(Y, EY_AHEAD, 0)
+        edge_pass(Y, EY_AHEAD, 1)
         for u in range(UNITS):
             product(Y, u)
             if u in GROUPS[0]:
@@ -333,14 +346,12 @@ def tile_list_edge_field_torque_kernel(
             if u in TURNED:
                 turn(Y, u)
                 turned_out(u)
-            if u < FX_BANKS and u in EY_BANKS[EY_AHEAD:]:
-                later = EY_AHEAD + EY_BANKS[EY_AHEAD:].index(u)
-                edge_pass(Y, later, 0)
-                edge_pass(Y, later, 1)
+            if u < 2:
+                edge_pass(Y, u + 6, 0)
+                edge_pass(Y, u + 6, 1)
             if u == GROUPS[2][1]:
                 torque(0)
                 difference(u, nc.gpsimd)
-        product(X, LAST)
         torque(1)
         torque(2)
         difference(LAST - 1, nc.vector)

@@ -35,9 +35,9 @@ M_SPLIT = 48
 
 FX_BANKS = 4
 EY_AHEAD = 5
-EY_BANKS = (6, 7, 0, 1, 2, 3, 6, 7)
+EY_BANKS = (6, 7, 0, 1, 2, 6, 7, 1)
 SUM_BANKS = {2: 4, 3: 5, 4: 0}
-OUT_BANKS = ((4, 1), (5, 2), (0, 3), (6,), (7,))
+OUT_BANKS = ((4, 2), (5, 6), (0, 7), (1,), (3,))
 
 
 def tile_list_edge_field_torque_kernel(
@@ -84,8 +84,8 @@ def tile_list_edge_field_torque_kernel(
         h_bf = [h_all[:, W * slot : W * (slot + len(units))] for slot, units in zip((1, 4, 0, 0, 1), GROUPS)]
         prod = [
             [sb("prod_x%d" % u, [P, W], F32)[:] for u in range(UNITS // 2)]
-            + [we_raw[Y][0][:, j, :] for j in range(3)]
-            + [we_raw[Y][1][:, 0, :]],
+            + [we_raw[Y][0][:, j, :] for j in range(2)]
+            + [we_raw[Y][1][:, 0, :], h_all[:, 2 * W : 4 * W].bitcast(F32)],
             [sb("prod_y%d" % u, [P, W], F32)[:] for u in range(UNITS)],
         ]
         h_words = [sb("h_words%d" % g, [P, len(units) * C], U32) for g, units in enumerate(GROUPS)]
@@ -134,7 +134,8 @@ def tile_list_edge_field_torque_kernel(
         for a in range(2):
             nc.vector.memset(gv_scales[a][:].bitcast(I32), 0)
         nc.vector.memset(wt_s[:], 0)
-        make_identity(nc, ident[:])
+        nc.vector.memset(ident[:], 0.0)
+        make_identity(nc, ident[:], nomemset=True)
 
         load_words(v2_words, tab2_words, 0, 0, T2 // 2)
         nc.sync.dma_start(idx2[:], offs2)
@@ -170,13 +171,6 @@ def tile_list_edge_field_torque_kernel(
             nc.sync.dma_start(out=wt_s[r:P:32, :], in_=wt_scales[0, r:16:4, :].bitcast(I32))
         with nc.allow_non_contiguous_dma(reason="one value of tl to a partition"):
             nc.sync.dma_start(out=tl_col[:], in_=tl.rearrange("(c p) -> p c", p=P))
-
-        def cast_on_gpsimd(w, a, t0):
-            dst = we_bf[w][:, PACK * H * a : PACK * H * (a + 1)].rearrange("p (t m j) -> p t m j", t=PACK, j=PACK)
-            src = we_raw[w][a][:].rearrange("p j (m t) -> p t m j", t=PACK)
-            nc.gpsimd.tensor_scalar(
-                out=dst[:, t0 : t0 + 2], in0=src[:, t0 : t0 + 2], scalar1=1.0, scalar2=0.0, op0=ALU.mult, op1=ALU.add,
-            )
 
         def cast(w, a, t0, on_vector=False, m0=0, m1=P):
             dst = we_bf[w][:, PACK * H * a : PACK * H * (a + 1)].rearrange("p (t m j) -> p m j t", t=PACK, j=PACK)
@@ -318,16 +312,18 @@ def tile_list_edge_field_torque_kernel(
         quantize_we(X, H, H + H // 2)
         quantize_we(X, H + H // 2, 2 * H)
 
-        cast_on_gpsimd(Y, 0, 0)
+        cast(Y, 0, 0)
         cast(Y, 0, 2)
         cast(Y, 1, 0)
-        cast(Y, 1, 2)
+        cast(Y, 1, 2, on_vector=True, m1=M_SPLIT)
+        cast(Y, 1, 2, m0=M_SPLIT)
         for c0 in range(0, 2 * H, H // 2):
             quantize_we(Y, c0, c0 + H // 2)
 
         for u in range(UNITS):
             edge_pass(X, u, 1)
-            product(X, u)
+            if u < LAST:
+                product(X, u)
         for u in TURNED[:2]:
             turn(X, u)
         nc.scalar.activation(out=neg_tl[:], in_=tl_col[:], func=ACT.Copy, scale=-1.0)
@@ -335,8 +331,6 @@ def tile_list_edge_field_torque_kernel(
         for a in range(2):
             for u in range(EY_AHEAD):
                 edge_pass(Y, u, a)
-        edge_pass(Y, EY_AHEAD, 0)
-        edge_pass(Y, EY_AHEAD, 1)
         for u in range(UNITS):
             product(Y, u)
             if u in GROUPS[0]:
@@ -346,12 +340,14 @@ def tile_list_edge_field_torque_kernel(
             if u in TURNED:
                 turn(Y, u)
                 turned_out(u)
-            if u < 2:
-                edge_pass(Y, u + 6, 0)
-                edge_pass(Y, u + 6, 1)
+            if EY_BANKS[u] in EY_BANKS[EY_AHEAD:] and u < EY_AHEAD:
+                later = EY_AHEAD + EY_BANKS[EY_AHEAD:].index(EY_BANKS[u])
+                edge_pass(Y, later, 0)
+                edge_pass(Y, later, 1)
             if u == GROUPS[2][1]:
                 torque(0)
                 difference(u, nc.gpsimd)
+        product(X, LAST)
         torque(1)
         torque(2)
         difference(LAST - 1, nc.vector)

@@ -33,6 +33,8 @@ V_PLANES = (4, 8)
 
 M_SPLIT = 48
 
+FX_ON_VECTOR = (2, 3)
+
 FX_BANKS = 4
 EY_AHEAD = 5
 EY_BANKS = (6, 7, 0, 1, 2, 6, 7, 1)
@@ -148,13 +150,13 @@ def tile_list_edge_field_torque_kernel(
         load_wf_words(X)
         load_words(v2_words, tab2_words, 0, T2 // 2, T2)
         load_scale_rows_apart(v_scales, tab_scales)
-        load_words(v_words[0], tab_words, 0, 0, T // 4)
+        load_words(v_words[0], tab_words, 0, 0, T // 2)
         gather(picked, v2_scales, U8, idx2, 0, S)
         for w in (Y, X):
             to_tm_order(wf_scales[w], wf_scales_raw[w][:].bitcast(U8))
         nc.vector.tensor_copy(gv2_scales.bitcast(I32), picked[:, :S].bitcast(I32))
         move_field_scale_rows()
-        load_words(v_words[0], tab_words, 0, T // 4, T)
+        load_words(v_words[0], tab_words, 0, T // 2, T)
         load_words(v_words[1], tab_words, 1, 0, T)
         for w in (Y, X):
             to_tm_order(wf_words[w][:].bitcast(U16), wf_words_raw[w][:].bitcast(U16))
@@ -205,7 +207,10 @@ def tile_list_edge_field_torque_kernel(
                     out=bank[:], lhsT=gv2_words[:, cols].bitcast(FP8X4), lhsT_scale=gv2_scales[:, cols],
                     rhs=wf_words[w][:].bitcast(FP4X4), rhs_scale=wf_scales[w], start=True, stop=True,
                 )
-                nc.scalar.activation(out=f_sb[w][u][:], in_=bank[:], func=ACT.Copy, scale=-1.0 if w == X else 1.0)
+                if w == X and u in FX_ON_VECTOR:
+                    nc.vector.tensor_scalar(out=f_sb[w][u][:], in0=bank[:], scalar1=-1.0, scalar2=None, op0=ALU.mult)
+                else:
+                    nc.scalar.activation(out=f_sb[w][u][:], in_=bank[:], func=ACT.Copy, scale=-1.0 if w == X else 1.0)
                 return
             for t in range(PACK):
                 nc.tensor.matmul_mx(

@@ -33,13 +33,12 @@ V_PLANES = (4, 8)
 
 M_SPLIT = 48
 
-FX_ON_VECTOR = (2, 3)
+FX_ON_VECTOR = (3, 4)
 
-FX_BANKS = 4
 EY_AHEAD = 5
-EY_BANKS = (6, 7, 0, 1, 2, 6, 7, 1)
-SUM_BANKS = {2: 4, 3: 5, 4: 0}
-OUT_BANKS = ((4, 2), (5, 6), (0, 7), (1,), (3,))
+EY_BANKS = (2, 3, 4, 5, 6, 2, 3, 5)
+SUM_BANKS = {2: 0, 3: 1, 4: 4}
+OUT_BANKS = ((0, 6), (1, 2), (4, 3), (5,), (7,))
 
 
 def tile_list_edge_field_torque_kernel(
@@ -98,9 +97,11 @@ def tile_list_edge_field_torque_kernel(
             words = dram[a].rearrange("p t i -> p (t i)").bitcast(I32)
             nc.sync.dma_start(out=tile[:, c0:c1], in_=words[:, c0:c1])
 
-        def load_we(w, a):
+        def load_we(w, a, j0=0, j1=PACK):
             rows = (wex, wey)[w][512 * a : 512 * (a + 1), :]
-            nc.sync.dma_start(out=we_raw[w][a][:], in_=rows.rearrange("(p j) c -> p j c", j=PACK))
+            nc.sync.dma_start(
+                out=we_raw[w][a][:, j0:j1, :], in_=rows.rearrange("(p j) c -> p j c", j=PACK)[:, j0:j1, :],
+            )
 
         def load_wf_words(w):
             nc.sync.dma_start(out=wf_words_raw[w][:], in_=(wfx_words, wfy_words)[w][0].bitcast(I32))
@@ -144,12 +145,12 @@ def tile_list_edge_field_torque_kernel(
         load_scale_rows_apart(v2_scales, tab2_scales)
         load_scale_rows_apart(wf_scales_raw[Y], wfy_scales)
         load_scale_rows_apart(wf_scales_raw[X], wfx_scales)
-        nc.sync.dma_start(idx[:], offs)
         load_we(X, 0)
         load_wf_words(Y)
         load_wf_words(X)
         load_words(v2_words, tab2_words, 0, T2 // 2, T2)
         load_scale_rows_apart(v_scales, tab_scales)
+        nc.sync.dma_start(idx[:], offs)
         load_words(v_words[0], tab_words, 0, 0, T // 2)
         gather(picked, v2_scales, U8, idx2, 0, S)
         for w in (Y, X):
@@ -165,8 +166,9 @@ def tile_list_edge_field_torque_kernel(
         gather(picked[:, S:], v_scales, U8, idx, 0, S)
         move_edge_scale_rows(0)
         load_we(X, 1)
+        load_we(Y, 0, 0, 2)
         move_edge_scale_rows(1)
-        load_we(Y, 0)
+        load_we(Y, 0, 2, 4)
         load_we(Y, 1)
         load_words(wt_w, wt_words, 0, 0, N)
         for r in range(4):
@@ -197,11 +199,11 @@ def tile_list_edge_field_torque_kernel(
             return ap.rearrange("p (n t) -> p n t", n=C)
 
         def edge_bank(w, u):
-            return banks[(FX_BANKS + u) % UNITS if w == X else EY_BANKS[u]]
+            return banks[u if w == X else EY_BANKS[u]]
 
         def field(w, u):
             cols = slice(C * u, C * (u + 1))
-            bank = banks[u if w == Y else u % FX_BANKS]
+            bank = banks[u]
             if u in TURNED:
                 nc.tensor.matmul_mx(
                     out=bank[:], lhsT=gv2_words[:, cols].bitcast(FP8X4), lhsT_scale=gv2_scales[:, cols],

@@ -36,9 +36,9 @@ M_SPLIT = 48
 FX_ON_VECTOR = (3, 4)
 
 EY_AHEAD = 5
-EY_BANKS = (2, 3, 4, 5, 6, 2, 3, 5)
+EY_BANKS = (2, 3, 4, 5, 7, 6, 2, 3)
 SUM_BANKS = {2: 0, 3: 1, 4: 4}
-OUT_BANKS = ((0, 6), (1, 2), (4, 3), (5,), (7,))
+OUT_BANKS = ((5, 0), (1, 7), (4, 6), (2,), (3,))
 
 
 def tile_list_edge_field_torque_kernel(
@@ -81,12 +81,13 @@ def tile_list_edge_field_torque_kernel(
         ident = sb("ident", [P, P], F32)
         f_sb = [[sb("f_sb%d%d" % (w, u), [P, W], F32) for u in range(UNITS)] for w in range(2)]
 
-        h_all = sb("h_all", [P, 6 * W], BF16)
-        h_bf = [h_all[:, W * slot : W * (slot + len(units))] for slot, units in zip((1, 4, 0, 0, 1), GROUPS)]
+        ex_last = we_raw[Y][0][:, 2, :]
+        h_all = sb("h_all", [P, 5 * W], BF16)
+        h_bf = [h_all[:, W * slot : W * (slot + len(units))] for slot, units in zip((1, 3, 0, 0, 1), GROUPS)]
         prod = [
             [sb("prod_x%d" % u, [P, W], F32)[:] for u in range(UNITS // 2)]
             + [we_raw[Y][0][:, j, :] for j in range(2)]
-            + [we_raw[Y][1][:, 0, :], h_all[:, 2 * W : 4 * W].bitcast(F32)],
+            + [we_raw[Y][1][:, 0, :], we_bf[Y][:, 2 * PACK * H - 2 * W :].bitcast(F32)],
             [sb("prod_y%d" % u, [P, W], F32)[:] for u in range(UNITS)],
         ]
         h_words = [sb("h_words%d" % g, [P, len(units) * C], U32) for g, units in enumerate(GROUPS)]
@@ -247,10 +248,10 @@ def tile_list_edge_field_torque_kernel(
 
         def product(w, u):
             if u in TURNED:
-                nc.vector.tensor_tensor(out=prod[w][u], in0=edge_bank(w, u)[:], in1=f_sb[1 - w][u][:], op=ALU.mult)
+                nc.vector.tensor_tensor(out=prod[w][u], in0=f_sb[1 - w][u][:], in1=edge_bank(w, u)[:], op=ALU.mult)
                 return
             nc.vector.tensor_tensor(
-                out=as_nt(prod[w][u]), in0=bank_as_nt(edge_bank(w, u)), in1=as_nt(f_sb[1 - w][u][:]), op=ALU.mult,
+                out=as_nt(prod[w][u]), in0=as_nt(f_sb[1 - w][u][:]), in1=bank_as_nt(edge_bank(w, u)), op=ALU.mult,
             )
 
         def h_of(u):
@@ -321,9 +322,8 @@ def tile_list_edge_field_torque_kernel(
 
         cast(Y, 0, 0)
         cast(Y, 0, 2)
-        cast(Y, 1, 0)
-        cast(Y, 1, 2, on_vector=True, m1=M_SPLIT)
-        cast(Y, 1, 2, m0=M_SPLIT)
+        cast(Y, 1, 2)
+        cast(Y, 1, 0, on_vector=True)
         for c0 in range(0, 2 * H, H // 2):
             quantize_we(Y, c0, c0 + H // 2)
 
@@ -331,6 +331,8 @@ def tile_list_edge_field_torque_kernel(
             edge_pass(X, u, 1)
             if u < LAST:
                 product(X, u)
+        nc.scalar.activation(out=as_nt(ex_last), in_=bank_as_nt(edge_bank(X, LAST)), func=ACT.Copy)
+        nc.gpsimd.tensor_tensor(out=prod[X][LAST], in0=ex_last, in1=f_sb[Y][LAST][:], op=ALU.mult)
         for u in TURNED[:2]:
             turn(X, u)
         nc.scalar.activation(out=neg_tl[:], in_=tl_col[:], func=ACT.Copy, scale=-1.0)
@@ -338,6 +340,8 @@ def tile_list_edge_field_torque_kernel(
         for a in range(2):
             for u in range(EY_AHEAD):
                 edge_pass(Y, u, a)
+        edge_pass(Y, EY_AHEAD, 0)
+        edge_pass(Y, EY_AHEAD, 1)
         for u in range(UNITS):
             product(Y, u)
             if u in GROUPS[0]:
@@ -347,14 +351,12 @@ def tile_list_edge_field_torque_kernel(
             if u in TURNED:
                 turn(Y, u)
                 turned_out(u)
-            if EY_BANKS[u] in EY_BANKS[EY_AHEAD:] and u < EY_AHEAD:
-                later = EY_AHEAD + EY_BANKS[EY_AHEAD:].index(EY_BANKS[u])
-                edge_pass(Y, later, 0)
-                edge_pass(Y, later, 1)
+            if u < 2:
+                edge_pass(Y, u + 6, 0)
+                edge_pass(Y, u + 6, 1)
             if u == GROUPS[2][1]:
                 torque(0)
                 difference(u, nc.gpsimd)
-        product(X, LAST)
         torque(1)
         torque(2)
         difference(LAST - 1, nc.vector)

@@ -32,6 +32,7 @@ TURNED = (2, 3, 4)
 V_PLANES = (4, 8)
 
 M_SPLIT = 48
+M_SPLIT_Y = 32
 
 FX_ON_VECTOR = (3, 4)
 
@@ -322,8 +323,9 @@ def tile_list_edge_field_torque_kernel(
 
         cast(Y, 0, 0)
         cast(Y, 0, 2)
-        cast(Y, 1, 2)
+        cast(Y, 1, 2, m0=M_SPLIT_Y)
         cast(Y, 1, 0, on_vector=True)
+        cast(Y, 1, 2, on_vector=True, m1=M_SPLIT_Y)
         for c0 in range(0, 2 * H, H // 2):
             quantize_we(Y, c0, c0 + H // 2)
 

@@ -33,6 +33,7 @@ V_PLANES = (4, 8)
 
 M_SPLIT = 48
 M_SPLIT_Y = 32
+M_SPLIT_POOL = 96
 
 FX_ON_VECTOR = (3, 4)
 
@@ -321,8 +322,13 @@ def tile_list_edge_field_torque_kernel(
         quantize_we(X, H, H + H // 2)
         quantize_we(X, H + H // 2, 2 * H)
 
-        cast(Y, 0, 0)
+        nc.gpsimd.tensor_scalar(
+            out=we_bf[Y][:, : 2 * PACK * P].rearrange("p (t m j) -> p t m j", t=2, j=PACK)[:, :, :M_SPLIT_POOL],
+            in0=we_raw[Y][0][:].rearrange("p j (m t) -> p t m j", t=PACK)[:, :2, :M_SPLIT_POOL],
+            scalar1=1.0, scalar2=0.0, op0=ALU.mult, op1=ALU.add,
+        )
         cast(Y, 0, 2)
+        cast(Y, 0, 0, m0=M_SPLIT_POOL)
         cast(Y, 1, 2, m0=M_SPLIT_Y)
         cast(Y, 1, 0, on_vector=True)
         cast(Y, 1, 2, on_vector=True, m1=M_SPLIT_Y)

@@ -33,7 +33,7 @@ V_PLANES = (4, 8)
 
 M_SPLIT = 48
 M_SPLIT_Y = 32
-M_SPLIT_POOL = 96
+M_SPLIT_POOL = 64
 
 FX_ON_VECTOR = (3, 4)
 

from contextlib import ExitStack

import concourse.mybir as mybir
from concourse.masks import make_identity

K, K2, H, N, T, T2, S = 1024, 512, 512, 384, 4096, 2048, 1024
FLOPS = 2 * S * (2 * K * H + 2 * K2 * H + H * N)

F32 = mybir.dt.float32
BF16 = mybir.dt.bfloat16
I32 = mybir.dt.int32
U32 = mybir.dt.uint32
U16 = mybir.dt.uint16
U8 = mybir.dt.uint8
FP8X4 = mybir.dt.float8_e4m3fn_x4
FP4X4 = mybir.dt.float4_e2m1fn_x4
ALU = mybir.AluOpType
ACT = mybir.ActivationFunctionType

P = 128
PACK = 4
C = 128
W = C * PACK
UNITS = S // C
LAST = UNITS - 1
HALF = S // 2
NT = N // P
X, Y = 0, 1

GROUPS = ((0, 1), (2, 3), (4, 5), (6,), (7,))
TURNED = (2, 3, 4)
V_PLANES = (4, 8)

M_SPLIT = 48
M_SPLIT_Y = 32
M_SPLIT_POOL = 64

FX_ON_VECTOR = (3, 4)

EY_AHEAD = 5
EY_BANKS = (2, 3, 4, 5, 7, 6, 2, 3)
SUM_BANKS = {2: 0, 3: 1, 4: 4}
OUT_BANKS = ((5, 0), (1, 7), (4, 6), (2,), (3,))


def tile_list_edge_field_torque_kernel(
    tc, tab_words, tab_scales, tab2_words, tab2_scales, offs, offs2, wex, wey,
    wfx_words, wfx_scales, wfy_words, wfy_scales, wt_words, wt_scales, tl, out,
):
    nc = tc.nc
    with ExitStack() as ctx:
        keep = ctx.enter_context(tc.tile_pool(name="keep", bufs=1))
        psum = ctx.enter_context(tc.psum_pool(name="psum", bufs=1))
        banks = [psum.tile([P, W], F32, name="bank%d" % b) for b in range(8)]

        def sb(name, shape, dtype):
            return keep.tile(shape, dtype, name=name, align_bytes=64)

        idx = keep.tile([P, S // 16], U16, name="idx")
        idx2 = keep.tile([P, S // 16], U16, name="idx2")
        v_words = [sb("v_words%d" % a, [P, T], I32) for a in range(2)]
        v_scales = sb("v_scales", [P, T // 4], I32)
        v2_words = sb("v2_words", [P, T2], I32)
        v2_scales = sb("v2_scales", [P, T2 // 4], I32)
        gv_words = [sb("gv_words%d" % a, [P, S], U32) for a in range(2)]
        gv2_words = sb("gv2_words", [P, S], U32)
        picked = sb("picked", [P, 2 * S], U8)
        gv_scales = [sb("gv_scales%d" % a, [P, S], U8) for a in range(2)]
        wf_words_raw = [sb("wf_words_raw%d" % w, [P, H // 2], I32) for w in range(2)]
        wf_scales_raw = [sb("wf_scales_raw%d" % w, [P, H // 4], I32) for w in range(2)]
        wf_words = [sb("wf_words%d" % w, [P, 2 * H], U8) for w in range(2)]
        field_planes = sb("field_planes", [P, 2 * H + S], U8)
        wf_scales = [field_planes[:, H * w : H * (w + 1)] for w in range(2)]
        gv2_scales = field_planes[:, 2 * H :]
        we_raw = [[sb("we_raw%d%d" % (w, a), [P, PACK, H], F32) for a in range(2)] for w in range(2)]
        we_bf = [sb("we_bf%d" % w, [P, 2 * PACK * H], BF16) for w in range(2)]
        we_words = [sb("we_words%d" % w, [P, 2 * H], U32) for w in range(2)]
        we_scales = [sb("we_scales%d" % w, [P, 2 * H], U8) for w in range(2)]
        wt_w = sb("wt_w", [P, N], I32)
        wt_s = sb("wt_s", [P, N // 4], I32)
        tl_col = sb("tl_col", [P, NT], F32)
        neg_tl = sb("neg_tl", [P, NT], F32)
        ident = sb("ident", [P, P], F32)
        f_sb = [[sb("f_sb%d%d" % (w, u), [P, W], F32) for u in range(UNITS)] for w in range(2)]

        ex_last = we_raw[Y][0][:, 2, :]
        h_all = sb("h_all", [P, 5 * W], BF16)
        h_bf = [h_all[:, W * slot : W * (slot + len(units))] for slot, units in zip((1, 3, 0, 0, 1), GROUPS)]
        prod = [
            [sb("prod_x%d" % u, [P, W], F32)[:] for u in range(UNITS // 2)]
            + [we_raw[Y][0][:, j, :] for j in range(2)]
            + [we_raw[Y][1][:, 0, :], we_bf[Y][:, 2 * PACK * H - 2 * W :].bitcast(F32)],
            [sb("prod_y%d" % u, [P, W], F32)[:] for u in range(UNITS)],
        ]
        h_words = [sb("h_words%d" % g, [P, len(units) * C], U32) for g, units in enumerate(GROUPS)]
        h_scales = [sb("h_scales%d" % g, [P, len(units) * C], U8) for g, units in enumerate(GROUPS)]
        y_sb = [sb("y_sb%d" % g, [P, NT, len(units) * C], F32) for g, units in enumerate(GROUPS)]

        def load_words(tile, dram, a, c0, c1):
            words = dram[a].rearrange("p t i -> p (t i)").bitcast(I32)
            nc.sync.dma_start(out=tile[:, c0:c1], in_=words[:, c0:c1])

        def load_we(w, a, j0=0, j1=PACK):
            rows = (wex, wey)[w][512 * a : 512 * (a + 1), :]
            nc.sync.dma_start(
                out=we_raw[w][a][:, j0:j1, :], in_=rows.rearrange("(p j) c -> p j c", j=PACK)[:, j0:j1, :],
            )

        def load_wf_words(w):
            nc.sync.dma_start(out=wf_words_raw[w][:], in_=(wfx_words, wfy_words)[w][0].bitcast(I32))

        def load_scale_rows_apart(tile, dram):
            rows = dram.rearrange("a q t -> (a q) t").bitcast(I32)
            nc.sync.dma_start(out=tile[0 : P : P // rows.shape[0], :], in_=rows)

        def move_field_scale_rows():
            for r in range(1, 4):
                nc.sync.dma_start(
                    out=field_planes[r:P:32, :].bitcast(I32), in_=field_planes[8 * r : P : 32, :].bitcast(I32),
                )

        def move_edge_scale_rows(a):
            for r in range(4):
                first = 64 * a + 4 * r
                nc.sync.dma_start(
                    out=gv_scales[a][V_PLANES[a] + r : P : 32, :].bitcast(I32),
                    in_=picked[first : first + 3 * 16 + 1 : 16, S:].bitcast(I32),
                )

        def gather(dst, window, dtype, offsets, j0, j1):
            nc.vector.tensor_copy(dst[:, j0:j1], window[:].bitcast(dtype).indirect(offsets[:, j0 // 16 : j1 // 16]))

        def to_tm_order(dst, src):
            nc.vector.tensor_copy(
                out=dst.rearrange("p (t m) -> p t m", t=PACK), in_=src.rearrange("p (m t) -> p t m", t=PACK),
            )

        for tile in (v2_scales, wf_scales_raw[Y], wf_scales_raw[X], v_scales):
            nc.vector.memset(tile[:], 0)
        for a in range(2):
            nc.vector.memset(gv_scales[a][:].bitcast(I32), 0)
        nc.vector.memset(wt_s[:], 0)
        nc.vector.memset(ident[:], 0.0)
        make_identity(nc, ident[:], nomemset=True)

        load_words(v2_words, tab2_words, 0, 0, T2 // 2)
        nc.sync.dma_start(idx2[:], offs2)
        load_scale_rows_apart(v2_scales, tab2_scales)
        load_scale_rows_apart(wf_scales_raw[Y], wfy_scales)
        load_scale_rows_apart(wf_scales_raw[X], wfx_scales)
        load_we(X, 0)
        load_wf_words(Y)
        load_wf_words(X)
        load_words(v2_words, tab2_words, 0, T2 // 2, T2)
        load_scale_rows_apart(v_scales, tab_scales)
        nc.sync.dma_start(idx[:], offs)
        load_words(v_words[0], tab_words, 0, 0, T // 2)
        gather(picked, v2_scales, U8, idx2, 0, S)
        for w in (Y, X):
            to_tm_order(wf_scales[w], wf_scales_raw[w][:].bitcast(U8))
        nc.vector.tensor_copy(gv2_scales.bitcast(I32), picked[:, :S].bitcast(I32))
        move_field_scale_rows()
        load_words(v_words[0], tab_words, 0, T // 2, T)
        load_words(v_words[1], tab_words, 1, 0, T)
        for w in (Y, X):
            to_tm_order(wf_words[w][:].bitcast(U16), wf_words_raw[w][:].bitcast(U16))
        gather(gv2_words, v2_words, U32, idx2, 0, HALF)
        gather(gv2_words, v2_words, U32, idx2, HALF, S)
        gather(picked[:, S:], v_scales, U8, idx, 0, S)
        move_edge_scale_rows(0)
        load_we(X, 1)
        load_we(Y, 0, 0, 2)
        move_edge_scale_rows(1)
        load_we(Y, 0, 2, 4)
        load_we(Y, 1)
        load_words(wt_w, wt_words, 0, 0, N)
        for r in range(4):
            nc.sync.dma_start(out=wt_s[r:P:32, :], in_=wt_scales[0, r:16:4, :].bitcast(I32))
        with nc.allow_non_contiguous_dma(reason="one value of tl to a partition"):
            nc.sync.dma_start(out=tl_col[:], in_=tl.rearrange("(c p) -> p c", p=P))

        def cast(w, a, t0, on_vector=False, m0=0, m1=P):
            dst = we_bf[w][:, PACK * H * a : PACK * H * (a + 1)].rearrange("p (t m j) -> p m j t", t=PACK, j=PACK)
            src = we_raw[w][a][:].rearrange("p j (m t) -> p m j t", t=PACK)
            if on_vector:
                nc.vector.tensor_copy(out=dst[:, m0:m1, :, t0 : t0 + 2], in_=src[:, m0:m1, :, t0 : t0 + 2])
            else:
                nc.scalar.activation(
                    out=dst[:, m0:m1, :, t0 : t0 + 2], in_=src[:, m0:m1, :, t0 : t0 + 2], func=ACT.Copy,
                )

        def quantize_we(w, c0, c1):
            nc.vector.quantize_mx(
                out=we_words[w][:, c0:c1].bitcast(FP8X4), scales=we_scales[w][:, c0:c1],
                in_=we_bf[w][:, PACK * c0 : PACK * c1],
            )

        def bank_as_nt(bank):
            return bank[:].rearrange("p (t n) -> p n t", n=C)

        def as_nt(ap):
            return ap.rearrange("p (n t) -> p n t", n=C)

        def edge_bank(w, u):
            return banks[u if w == X else EY_BANKS[u]]

        def field(w, u):
            cols = slice(C * u, C * (u + 1))
            bank = banks[u]
            if u in TURNED:
                nc.tensor.matmul_mx(
                    out=bank[:], lhsT=gv2_words[:, cols].bitcast(FP8X4), lhsT_scale=gv2_scales[:, cols],
                    rhs=wf_words[w][:].bitcast(FP4X4), rhs_scale=wf_scales[w], start=True, stop=True,
                )
                if w == X and u in FX_ON_VECTOR:
                    nc.vector.tensor_scalar(out=f_sb[w][u][:], in0=bank[:], scalar1=-1.0, scalar2=None, op0=ALU.mult)
                else:
                    nc.scalar.activation(out=f_sb[w][u][:], in_=bank[:], func=ACT.Copy, scale=-1.0 if w == X else 1.0)
                return
            for t in range(PACK):
                nc.tensor.matmul_mx(
                    out=bank[:, C * t : C * (t + 1)],
                    lhsT=wf_words[w][:, 2 * P * t : 2 * P * (t + 1)].bitcast(FP4X4),
                    lhsT_scale=wf_scales[w][:, P * t : P * (t + 1)],
                    rhs=gv2_words[:, cols].bitcast(FP8X4),
                    rhs_scale=gv2_scales[:, cols],
                    start=True, stop=True,
                )
            nc.scalar.activation(out=as_nt(f_sb[w][u][:]), in_=bank_as_nt(bank), func=ACT.Copy)

        def edge_pass(w, u, a):
            cols = slice(C * u, C * (u + 1))
            entries = gv_words[a][:, cols].bitcast(FP8X4)
            entry_scales = gv_scales[a][V_PLANES[a] : P, cols]
            if u in TURNED:
                nc.tensor.matmul_mx(
                    out=edge_bank(w, u)[:], lhsT=entries, lhsT_scale=entry_scales,
                    rhs=we_words[w][:, H * a : H * (a + 1)].bitcast(FP8X4), rhs_scale=we_scales[w][:, H * a : H * (a + 1)],
                    start=(a == 0), stop=(a == 1),
                )
                return
            for t in range(PACK):
                wcols = slice(H * a + P * t, H * a + P * (t + 1))
                nc.tensor.matmul_mx(
                    out=edge_bank(w, u)[:, C * t : C * (t + 1)],
                    lhsT=we_words[w][:, wcols].bitcast(FP8X4), lhsT_scale=we_scales[w][:, wcols],
                    rhs=entries, rhs_scale=entry_scales,
                    start=(a == 0 and t == 0), stop=(a == 1 and t == PACK - 1),
                )

        def product(w, u):
            if u in TURNED:
                nc.vector.tensor_tensor(out=prod[w][u], in0=f_sb[1 - w][u][:], in1=edge_bank(w, u)[:], op=ALU.mult)
                return
            nc.vector.tensor_tensor(
                out=as_nt(prod[w][u]), in0=as_nt(f_sb[1 - w][u][:]), in1=bank_as_nt(edge_bank(w, u)), op=ALU.mult,
            )

        def h_of(u):
            g = [u in units for units in GROUPS].index(True)
            first = W * GROUPS[g].index(u)
            return h_bf[g][:, first : first + W]

        def turn(w, u):
            for t in range(PACK):
                nc.tensor.matmul(
                    banks[SUM_BANKS[u]][:, C * t : C * (t + 1)], lhsT=prod[w][u][:, P * t : P * (t + 1)], rhs=ident[:],
                    start=(w == X and t == 0), stop=(w == Y and t == PACK - 1), is_transpose=True,
                )

        def turned_out(u):
            nc.scalar.activation(out=as_nt(h_of(u)), in_=bank_as_nt(banks[SUM_BANKS[u]]), func=ACT.Copy)

        def difference(u, engine):
            engine.tensor_tensor(out=h_of(u), in0=prod[X][u], in1=prod[Y][u], op=ALU.subtract)

        def torque(g, on_vector=False):
            units = GROUPS[g]
            width = C * len(units)
            cols = slice(C * units[0], C * units[0] + width)
            nc.vector.quantize_mx(out=h_words[g][:].bitcast(FP8X4), scales=h_scales[g][:], in_=h_bf[g])
            sums = []
            for i in range(NT):
                b, first = divmod(width * i, W)
                sums.append(banks[OUT_BANKS[g][b]][:, first : first + width])
                nc.tensor.matmul_mx(
                    out=sums[i],
                    lhsT=wt_w[:, P * i : P * (i + 1)].bitcast(FP8X4),
                    lhsT_scale=wt_s[:].bitcast(U8)[:, P * i : P * (i + 1)],
                    rhs=h_words[g][:].bitcast(FP8X4),
                    rhs_scale=h_scales[g][:],
                    start=True, stop=True,
                )
            for i in range(NT):
                if on_vector:
                    nc.vector.tensor_scalar(
                        out=y_sb[g][:, i, :], in0=sums[i], scalar1=tl_col[:, i : i + 1], scalar2=None, op0=ALU.subtract,
                    )
                else:
                    nc.scalar.activation(
                        out=y_sb[g][:, i, :], in_=sums[i], func=ACT.Identity, bias=neg_tl[:, i : i + 1], scale=1.0,
                    )
                if len(units) > 1:
                    nc.sync.dma_start(out=out[P * i : P * (i + 1), cols], in_=y_sb[g][:, i, :])
            if len(units) == 1:
                nc.sync.dma_start(out=out.rearrange("(i p) n -> p i n", p=P)[:, :, cols], in_=y_sb[g][:])

        cast(X, 0, 0)
        cast(X, 0, 2)
        for w in (Y, X):
            for u in range(UNITS):
                field(w, u)
        quantize_we(X, 0, H)

        gather(gv_words[0], v_words[0], U32, idx, 0, S)
        for u in range(UNITS):
            edge_pass(X, u, 0)
        gather(gv_words[1], v_words[1], U32, idx, 0, S)
        cast(X, 1, 0, on_vector=True)
        cast(X, 1, 2, on_vector=True, m1=M_SPLIT)
        cast(X, 1, 2, m0=M_SPLIT)
        quantize_we(X, H, H + H // 2)
        quantize_we(X, H + H // 2, 2 * H)

        nc.gpsimd.tensor_scalar(
            out=we_bf[Y][:, : 2 * PACK * P].rearrange("p (t m j) -> p t m j", t=2, j=PACK)[:, :, :M_SPLIT_POOL],
            in0=we_raw[Y][0][:].rearrange("p j (m t) -> p t m j", t=PACK)[:, :2, :M_SPLIT_POOL],
            scalar1=1.0, scalar2=0.0, op0=ALU.mult, op1=ALU.add,
        )
        cast(Y, 0, 2)
        cast(Y, 0, 0, m0=M_SPLIT_POOL)
        cast(Y, 1, 2, m0=M_SPLIT_Y)
        cast(Y, 1, 0, on_vector=True)
        cast(Y, 1, 2, on_vector=True, m1=M_SPLIT_Y)
        for c0 in range(0, 2 * H, H // 2):
            quantize_we(Y, c0, c0 + H // 2)

        for u in range(UNITS):
            edge_pass(X, u, 1)
            if u < LAST:
                product(X, u)
        nc.scalar.activation(out=as_nt(ex_last), in_=bank_as_nt(edge_bank(X, LAST)), func=ACT.Copy)
        nc.gpsimd.tensor_tensor(out=prod[X][LAST], in0=ex_last, in1=f_sb[Y][LAST][:], op=ALU.mult)
        for u in TURNED[:2]:
            turn(X, u)
        nc.scalar.activation(out=neg_tl[:], in_=tl_col[:], func=ACT.Copy, scale=-1.0)

        for a in range(2):
            for u in range(EY_AHEAD):
                edge_pass(Y, u, a)
        edge_pass(Y, EY_AHEAD, 0)
        edge_pass(Y, EY_AHEAD, 1)
        for u in range(UNITS):
            product(Y, u)
            if u in GROUPS[0]:
                difference(u, nc.gpsimd)
            if u == TURNED[-1]:
                turn(X, u)
            if u in TURNED:
                turn(Y, u)
                turned_out(u)
            if u < 2:
                edge_pass(Y, u + 6, 0)
                edge_pass(Y, u + 6, 1)
            if u == GROUPS[2][1]:
                torque(0)
                difference(u, nc.gpsimd)
        torque(1)
        torque(2)
        difference(LAST - 1, nc.vector)
        difference(LAST, nc.vector)
        torque(3, on_vector=True)
        torque(4)
